import numpy as np, ml_dtypes
CORES = [40,64,80,88,96,104,120,144]
N = 8
BF = ml_dtypes.bfloat16
V, NF, NS, J, AM, RO = 256, 4096, 1024, 11, 127, 3
NV = N * V
def parts(rng):
    x = rng.integers(0, 256, (N, 8, 16, V)); y = rng.integers(0, 256, (N, 8, 16, NF)); f = rng.integers(0, NF, (N, 8, 16, NS))
    c = rng.integers(0, NV, (N, 8, 16, V)); e = rng.integers(0, NS, (N, 8, V))
    th = rng.integers(1180, 1440, (N, 8, 1)) + rng.integers(-60, 61, (N, 8, 16))
    return x, y, f, c, e, th
def halves(rng, n, edge, w):
    x = rng.integers(0, w, (N, 8, 16, V)); h = NF // 2; s = rng.integers(0, 2, (N, 8, h)); m = np.zeros((N, 8, NF), np.int64)
    m[..., 0::2] = s; m[..., 1::2] = 1 - s
    y = rng.integers(0, w, (N, 8, 16, NF)) + (256 - w) * m[:, :, None, :]
    r = (np.argsort(rng.random((N, 8, 16, NS)), axis=2) < n[:, :, None, :]).astype(np.int64)
    u = rng.integers(0, h, r.shape); u = np.where(rng.random(r.shape) < edge, (h - 1) * rng.integers(0, 2, r.shape), u)
    f = 2 * u + (np.take_along_axis(s, u.reshape(N, 8, -1), 2).reshape(u.shape) ^ r)
    return x, y, f
def pack(x, y, f, c, e, th):
    return {"x0": np.ascontiguousarray(x.reshape(N, 128, V)).astype(np.float32).astype(BF), "frm": np.ascontiguousarray(y.reshape(N, 128, NF)).astype(np.float32).astype(BF),
            "rol": np.ascontiguousarray(f.reshape(N, 128, NS)).astype(np.int32), "cas": np.ascontiguousarray(c.reshape(N, 128, V)).astype(np.int32),
            "sc0": np.ascontiguousarray(e).astype(np.int32), "th": np.ascontiguousarray(th.reshape(N, 128, 1)).astype(np.int32)}
def setup_inputs(rng):
    return pack(*parts(rng))
def setup_inputs_spread(rng):
    x, y, f, c, e, th = parts(rng); w = rng.choice(np.array([1.0, 2.0, 4.0]), (N, 8, 1, 1))
    x = (rng.random(x.shape) * np.exp2(rng.integers(0, 9, (N, 8, 1, V)))).astype(np.int64)
    y = (rng.random(y.shape) * np.exp2(rng.integers(0, 9, (N, 8, 1, NF)))).astype(np.int64)
    f = np.minimum((NF * rng.random(f.shape) ** w).astype(np.int64), NF - 1); c = NV - 1 - np.minimum((NV * rng.random(c.shape) ** w).astype(np.int64), NV - 1)
    e = np.minimum((NS * rng.random(e.shape) ** w[..., 0]).astype(np.int64), NS - 1)
    th = np.minimum((4080 * rng.random((N, 8, 1)) ** 2 * rng.random((N, 8, 16))).astype(np.int64), 4079)
    return pack(x, y, f, c, e, th)
def setup_inputs_ends(rng):
    x, y, f, c, e, th = parts(rng); k = np.arange(16)
    def flat(n):
        return 255 * np.where(rng.random((N, 8, 1, n)) < 0.5, rng.integers(0, 2, (N, 8, 1, n)), rng.integers(0, 2, (N, 8, 16, n)))
    x, y = flat(V), flat(NF)
    y[..., 0] = 255 * rng.integers(0, 2, (N, 8, 1)); y[..., NF - 1] = 255 - y[..., 0]
    x[0, :, :, 0] = 255 * rng.integers(0, 2, (8, 1)); x[N - 1, :, :, V - 1] = 255 * rng.integers(0, 2, (8, 1))
    f = np.where(rng.random(f.shape) < 0.85, (NF - 1) * rng.integers(0, 2, f.shape), f)
    c = np.where(rng.random(c.shape) < 0.85, (NV - 1) * rng.integers(0, 2, c.shape), c)
    e = np.where(rng.random(e.shape) < 0.85, (NS - 1) * rng.integers(0, 2, e.shape), e)
    th = 4079 * (rng.random((N, 8, 16)) < rng.choice(np.array([0.0, 0.25, 0.5, 1.0]), (N, 8, 1))).astype(np.int64)
    th[:, 7] = 4079 * ((k & 3) == 3)
    y[:, 7, :, 0] = 0; y[:, 7, :, NF - 1] = 255; x[0, 7, :, 0] = 0; x[N - 1, 7, :, V - 1] = 255; f[:, 7, :, NS - 1] = (NF - 1) * (k & 1)
    y[:, 6, :, 0] = 255; y[:, 6, :, NF - 1] = 255; x[0, 6, :, 0] = 0; x[N - 1, 6, :, V - 1] = 0; f[:, 6, :, NS - 1] = (NF - 1) * (1 - (k & 1))
    for g in (6, 7):
        c[:, g, :, V - 2:] = ((NV - 1) * ((k >> 1) & 1))[:, None]; e[:, g, V - 2:] = NS - 1
    return pack(x, y, f, c, e, th)
def setup_inputs_corners(rng):
    x, y, f, c, e, th = parts(rng); n = rng.choice(np.array([0, 1, J - 1, J, J + 1, 15, 16]), (N, 8, NS))
    n[..., 0] = J - 1; n[..., NS - 1] = J; n[..., NS - 2] = J - 1; n[::2, ::2, 0] = J; n[::2, 1::2, NS - 1] = J - 1
    x, y, f = halves(rng, n, 0.2, 8)
    e = np.where(rng.random(e.shape) < 0.5, rng.choice(np.array([0, 1, NS - 2, NS - 1]), e.shape), e)
    me = (np.arange(N)[:, None] * V + np.arange(V))[:, None, None, :]; kind = ((np.arange(N)[:, None] + np.arange(8)) & 3)[:, :, None, None]
    own = np.where(rng.random(c.shape) < 0.5, me, c); nxt = (me + 1 + np.arange(16)[:, None]) % NV; few = rng.choice(np.array([0, V - 1, NV - V, NV - 1]), c.shape)
    c = np.where(kind == 0, own, np.where(kind == 1, nxt, np.where(kind == 2, few, c)))
    return pack(x, y, f, c, e, rng.integers(300, 1600, (N, 8, 16)))
def setup_inputs_crowd(rng):
    x, y, f, c, e, th = parts(rng); a, g = np.arange(N)[:, None], np.arange(8)[None, :]
    part = ((a >= 2) & ((a & 1) == 0))[:, :, None]
    sp = rng.integers(0, NS, (N, 8, 1)); n = rng.integers(15, 17, (N, 8, NS))
    n = np.where(((a >= 2) & ((g & 1) == 1))[:, :, None], rng.integers(0, 17, n.shape), n); np.put_along_axis(n, sp, J - 1, 2)
    bit = rng.integers(0, 2, (N, 8, NS // 2)); strong = np.zeros((N, 8, NS), np.int64); strong[..., 0::2] = bit; strong[..., 1::2] = 1 - bit
    n = np.where(part, np.where(strong == 1, rng.integers(15, 17, n.shape), rng.integers(0, J, n.shape)), n)
    x, y, f = halves(rng, n, 0.1, 4)
    e = np.where((g & 1)[:, :, None] == 0, (sp + 1) & (NS - 1), (sp + 1 + rng.integers(0, NS - 1, (N, 8, V))) & (NS - 1))
    hit = rng.integers(0, 2, (N, 8, V))
    for q in range(2, N, 2):
        m = (AM + 1) * (1 + 2 * int(rng.integers(0, 2 * V // (AM + 1))))
        o = np.argsort((rng.random((8, V // 2)) + rng.random((8, 1))).reshape(-1)); z = np.zeros(4 * V, np.int64); z[o[:m]] = 1
        hit[q, :, 0::2] = z.reshape(8, V // 2)
    u = rng.integers(0, NS // 2, (N, 8, V)); e = np.where(part, 2 * u + (np.take_along_axis(bit, u, 2) ^ hit), e)
    less = rng.random((N, 8)) < 0.5; less[0] = False; less[1] = False; less[2::2] = False; less[1, rng.integers(0, 8)] = True; less[3, 7] = True
    at = 2 * rng.integers(0, V // 2, (N, 8)); at[:, 7] = V - 2
    for q in range(N):
        for j in range(8):
            if less[q, j]: e[q, j, at[q, j]:at[q, j] + 2] = sp[q, j, 0]
    three = np.take_along_axis(rng.integers(0, NV, (N, 8, 3)), rng.integers(0, 3, (N, 8, 16 * V)), 2).reshape(c.shape)
    kind = (g & 3)[:, :, None, None]; one = rng.integers(0, NV, (1, 8, 1, 1))
    c = np.where(kind == 0, one, np.where(kind == 1, three, c)); c[1::2, 0::4, 15, V - 1] = rng.integers(0, NV, c[1::2, 0::4, 15, V - 1].shape)
    loose = np.argsort(rng.random((N, 8, 16)), axis=2) < min(4, 15 - J)
    th = np.where(loose, rng.integers(4024, 4041, (N, 8, 16)), rng.integers(4080 - AM, 3984, (N, 8, 16)))
    low = (((g & 3) == 1) & (a != 1))[:, :, None]
    return pack(x, y, f, c, e, np.where(low, rng.integers(300, 1600, (N, 8, 16)), th))
def setup_inputs_ties(rng):
    x, y, f, c, e, th = parts(rng); pt = rng.integers(0, 16, (8, 16, 1))
    x = 20 * rng.integers(0, 13, (N, 8, 1, V)) + pt; y = 20 * rng.integers(0, 13, (N, 8, 1, NF)) + pt
    th = 320 * rng.integers(2, 6, (N, 8, 1)) + rng.integers(-1, 2, (N, 8, 16))
    return pack(x, y, f, c, e, th)
def check_inputs(d):
    bad = []
    for k, lo, hi in (("x0", 0, 255), ("frm", 0, 255), ("rol", 0, NF - 1), ("cas", 0, NV - 1), ("sc0", 0, NS - 1), ("th", 0, 4079)):
        v = np.asarray(d[k]).astype(np.float64)
        if not (np.min(v) >= lo and np.max(v) <= hi): bad.append("range of " + k)
        elif np.any(v != np.floor(v)): bad.append("whole numbers in " + k)
    return bad
def reference(x0, frm, rol, cas, sc0, th):
    x = x0.astype(np.float32).astype(np.int64).reshape(N, 8, 16, V); y = frm.astype(np.float32).astype(np.int64).reshape(N, 8, 16, NF)
    f = rol.astype(np.int64).reshape(N, 8, 16, NS); c = cas.astype(np.int64).reshape(N, 8, 16, V); e = sc0.astype(np.int64).reshape(N, 8, V)
    lim = th.astype(np.int64).reshape(N, 8, 16, 1); jumps = np.zeros(N, np.int64)
    for t in range(RO):
        own = np.arange(t & 1, V, 2)
        xa = np.array(x.transpose(1, 2, 0, 3)).reshape(8, 16, NV); ca = np.array(c.transpose(1, 2, 0, 3)).reshape(8, 16, NV)
        for a in range(N):
            ev = e[a][:, own]; ck = c[a][:, :, own]; fk = np.take_along_axis(f[a], ev[:, None, :], 2)
            yk = np.take_along_axis(y[a], fk.reshape(8, 1, -1), 2).reshape(8, 16, 16, -1); xk = np.take_along_axis(xa, ck.reshape(8, 1, -1), 2).reshape(8, 16, 16, -1)
            dist = np.add.reduce(np.abs(yk - xk), axis=1)
            b = np.argmin(dist, axis=1)[:, None, :]
            rej = dist > lim[a] + (jumps[a] & AM)
            jump = np.add.reduce(rej.astype(np.int64), axis=1)[:, None, :] >= J
            fb = np.take_along_axis(fk, b, 1); cb = np.take_along_axis(ck, b, 1)
            yb = np.take_along_axis(y[a], fb, 2); cc = np.take_along_axis(ca, cb, 2); xo = xa[:, :, a * V + own]
            x[a][:, :, own] = np.where(jump, (xo + yb) >> 1, np.abs(xo - yb))
            c[a][:, :, own] = np.where(rej & ~jump, cc, ck)
            e[a][:, own] = np.where(jump, fb & (NS - 1), (ev[:, None, :] + 1) & (NS - 1))[:, 0]
            jumps[a] = np.add.reduce(jump.reshape(-1).astype(np.int64))
    return {"yx": x.reshape(N, 128, V).astype(np.float32).astype(BF), "yc": c.reshape(N, 128, V).astype(np.float32), "ye": e.astype(np.float32)}

@@ -1,0 +1,564 @@
+from concourse.bass import DstId, RemoteDMATransfer
+from concourse.mybir import AluOpType as OP, AxisListType, ActivationFunctionType as AF
+
+NR, V, H = 8, 256, 128
+UE, UO = 2048, 3072
+WIN = [(0, 2048), (0, 3072), (2048, 4096)]
+CHUNKS = [(0, 16), (16, 40), (40, 64), (64, 88), (88, 104), (104, 120), (120, 128)]
+YV = 40
+FCUT = 3072
+ROLES = {64: [(0, 0, 6)], 88: [(0, 6, 10)], 104: [(0, 10, 12)], 128: [(0, 12, 16), (64, 0, 16)]}
+X0 = 0
+KW = 2048.0
+
+F, B, I, U = "float32", "bfloat16", "int32", "uint16"
+
+
+def _sb(n, d):
+    return ("sbuf", [128, n], d)
+
+
+SCRATCH = {
+    "dx": ("dram", [128, 256], B), "cu": _sb(2048, U),
+    "xt": _sb(4096, B), "ct": _sb(4096, F), "fr": _sb(4096, B), "ro": _sb(1024, I), "ca": _sb(256, I),
+    "ei": _sb(16, I), "ti": _sb(1, I),
+    "yg": _sb(2048, B), "df": _sb(2048, B), "ad": _sb(2048, B),
+    "col": _sb(144, I), "pi": _sb(8, I), "pf": _sb(16, F), "lf": _sb(40, F), "lu": _sb(40, U),
+    "b16": _sb(144, B), "gpw": _sb(128, B), "gmw": _sb(128, B), "vpw": _sb(128, B), "vmw": _sb(128, B),
+    "ones": _sb(128, B), "kp": _sb(128, B), "kb": _sb(128, B), "cst": _sb(512, B), "rst": _sb(128, B),
+    "ki": _sb(128, I), "cg": _sb(128, I), "t1": _sb(128, F), "t2": _sb(128, F),
+    "sl": _sb(48, U), "e1": _sb(48, I), "en0": _sb(8, F), "bias": _sb(4, F),
+    "ofr": _sb(256, U), "oxt": _sb(256, U), "cp": _sb(128, F),
+    "xf": _sb(256, F), "xc": _sb(256, F), "tf": _sb(256, F), "tc": _sb(256, F), "pw": _sb(528, F), "dl": _sb(512, F),
+    "u1": _sb(128, I), "u2": _sb(128, I), "u3": _sb(128, F), "u4": _sb(128, F), "u5": _sb(128, F),
+    "xoh": _sb(128, B), "xoq": _sb(128, F),
+    "mn": _sb(128, F), "nn": _sb(128, F), "zz": _sb(256, F), "bi": _sb(16, I), "bu": _sb(24, U), "mi": _sb(16, I),
+    "sg": _sb(128, B), "ybj": _sb(128, B), "ddh": _sb(128, B), "aa": _sb(128, B), "hh": _sb(128, I),
+    "p2": _sb(128, B), "vps": _sb(128, F), "ccj": _sb(128, F), "q1": _sb(128, F),
+    "j01": _sb(8, B), "fm": _sb(8, I), "ed": _sb(16, F), "as1": _sb(1, F), "ai": _sb(2, I),
+    "outx": _sb(256, B), "outc": _sb(256, F), "oute": _sb(16, F),
+    "key": ("psum", [128, 512], F), "dr": ("psum", [128, 512], F), "gp": ("psum", [128, 512], F),
+    "gm": ("psum", [128, 512], F), "vp": ("psum", [128, 512], F), "vm": ("psum", [128, 512], F),
+    "jw": ("psum", [128, 512], F), "at": ("psum", [128, 512], F),
+}
+PHASES = ["x0", "c0", "x1", "c1", "x2", "c2"]
+SEMAPHORES = (["qv", "qa", "qp", "qg", "go", "sent", "lx", "lc", "le", "lt", "lr", "ld", "lf1", "lf2", "ox", "oc", "oe"]
+              + ["a" + p for p in PHASES] + ["h" + p for p in PHASES])
+PSUM = [n for n in SCRATCH if SCRATCH[n][0] == "psum"]
+COUNTER = {"v": "qv", "a": "qa", "p": "qp", "g": "qg"}
+
+
+def _block(phase, q):
+    name = "xt" if phase[0] == "x" else "ct"
+    t = int(phase[1])
+    if t == 0:
+        return "xt" if phase[0] == "x" else "cu", q * V, q * V + V
+    base = UE if t == 1 else UO
+    return name, base + q * H, base + q * H + H
+
+
+def _bits(engines):
+    m = 0
+    for e in engines:
+        m |= 1 << e
+    return m
+
+
+def _plan(T, topo, q):
+    me = T.cores[q]
+    others = [T.cores[(q + d) % NR] for d in range(1, NR)]
+    near = [c for c in others if topo.may_write(me, c)]
+    far = [c for c in T.cores if c != me and not topo.may_write(me, c)]
+    turn = len([c for c in near if T.rank_of(c) < q]) % len(far)
+    far = far[turn:] + far[:turn]
+    free = [c for c in topo.cores_of(me) if T.rank_of(c) is None]
+    able = [c for c in free if all(topo.may_write(c, d) for d in far)]
+    able.sort(key=lambda c: topo.die(c) == topo.die(me))
+    hf = able[:2]
+    rest = [c for c in free if c not in hf]
+    rest.sort(key=lambda c: topo.die(c) != topo.die(me))
+    hn = rest[:2]
+    plan = {}
+    for p in PHASES:
+        relays = [(hf[0], far[0::2]), (hf[1], far[1::2])]
+        direct = near
+        if p == "x0" and X0 == 0:
+            relays = relays + [(hn[0], near[0::2]), (hn[1], near[1::2])]
+            direct = []
+        if p == "x0" and X0 == 1:
+            relays = [(able[i], [far[i]]) for i in range(len(far))]
+        plan[p] = (direct, relays)
+    return plan
+
+
+def _dst(topo, d, s):
+    rid, pid = topo.addr(d, s)
+    return DstId(rid=rid, pnc=pid)
+
+
+def _first_hop(T, topo, q, p):
+    me = T.cores[q]
+    direct, relays = _plan(T, topo, q)[p]
+    on = topo.engines(me, relays[0][0])
+    hands = [h for h, d in relays]
+    if not direct:
+        return [[(hands, on, "h" + p)]]
+    off = topo.engines(me, direct[0])
+    if p[0] == "x":
+        return [[(hands, on, "h" + p)], [(direct, off, "a" + p)]]
+    return [[(direct, off, "a" + p), (hands, [e for e in on if e not in off], "h" + p)]]
+
+
+def _arrivals(T, topo, q, p):
+    me, n = T.cores[q], 0
+    for s in range(NR):
+        if s == q:
+            continue
+        for call in _first_hop(T, topo, s, p):
+            for dsts, eng, sem in call:
+                if me in dsts:
+                    n += len(eng)
+        for h, dsts in _plan(T, topo, s)[p][1]:
+            if me in dsts:
+                n += len(topo.engines(h, me))
+    return n
+
+
+def _sides(T, p, q):
+    name, lo, hi = _block(p, q)
+    return (T.dx[:] if p == "x0" else T[name][:, lo:hi]), T[name][:, lo:hi]
+
+
+def _relay(g, core, T, topo):
+    own = [c for c in topo.cores_of(core) if T.rank_of(c) is not None]
+    if not own:
+        return
+    q = T.rank_of(own[0])
+    plan, sent = _plan(T, topo, q), 0
+    for p in PHASES:
+        for h, dsts in plan[p][1]:
+            if h != core:
+                continue
+            got = [len(e) for call in _first_hop(T, topo, q, p) for d, e, s in call if core in d][0]
+            here, there = _sides(T, p, q)
+            eng = topo.engines(core, dsts[0])
+            g.wait_ge(T.sem["h" + p], got)
+            g.remote_dma_fused([RemoteDMATransfer(
+                dst_ids=[_dst(topo, d, core) for d in dsts], dma_engine_mask=_bits(eng), remote_sem=T.sem["a" + p],
+                srcs=[here], dsts=[there for d in dsts])], local_sem=T.sem.sent)
+            sent += len(eng)
+    if sent:
+        g.wait_ge(T.sem.sent, sent)
+
+
+def _emit(ops, g, T):
+    queue = {"v": g.vector, "a": g.scalar, "p": g.tensor, "g": g, "s": g.sync}
+    known = {k: {} for k in queue}
+    seen = {}
+    for n, o in enumerate(ops):
+        deps = set(o["after"])
+        for wr, views in ((False, o["r"]), (True, o["w"])):
+            for name, lo, hi in views:
+                for m, w2, l2, h2 in seen.get(name, []):
+                    same = ops[m]["q"] == o["q"] and ops[m]["sem"] is None
+                    if name in PSUM:
+                        if not same or (o["q"] != "p" and (wr or w2)):
+                            deps.add(m)
+                    elif (wr or w2) and lo < h2 and l2 < hi:
+                        deps.add(m)
+        deps.discard(n)
+        for wr, views in ((False, o["r"]), (True, o["w"])):
+            for name, lo, hi in views:
+                seen.setdefault(name, []).append((n, wr, lo, hi))
+        o["src"] = o["sem"] if o["sem"] else o["q"]
+        o["waits"] = []
+        if o["q"] is None:
+            o["clock"] = {o["src"]: n}
+            continue
+        k = known[o["q"]]
+        for m in sorted(deps, reverse=True):
+            if k.get(ops[m]["src"], -1) < m:
+                o["waits"].append(m)
+                ops[m]["need"] = True
+                for s, x in ops[m]["clock"].items():
+                    k[s] = max(k.get(s, -1), x)
+        o["clock"] = dict(k)
+        o["clock"][o["src"]] = n
+    count = {k: 0 for k in COUNTER}
+    for o in ops:
+        if o["q"] is None:
+            continue
+        for m in o["waits"]:
+            queue[o["q"]].wait_ge(T.sem[ops[m]["ev"][0]], ops[m]["ev"][1])
+        ins = o["call"]()
+        if o["sem"] is None and o["need"]:
+            count[o["q"]] += 1
+            ins.then_inc(T.sem[COUNTER[o["q"]]], 1)
+            o["ev"] = (COUNTER[o["q"]], count[o["q"]])
+
+
+def rank_program(g, core, T, topo):
+    q = T.rank_of(core)
+    if q is None:
+        _relay(g, core, T, topo)
+        return
+    ops = []
+
+    def vw(name, lo=0, hi=None, st=1):
+        return (name, lo, SCRATCH[name][1][1] if hi is None else hi, st)
+
+    def ind(win, off):
+        return ("ind", win, off)
+
+    def ap(v):
+        if not isinstance(v, tuple):
+            return v
+        if v[0] == "ind":
+            return ap(v[1]).indirect(ap(v[2]))
+        return T[v[0]][:, v[1]:v[2]] if v[3] == 1 else T[v[0]][:, v[1]:v[2]:v[3]]
+
+    def spans(vs):
+        out = []
+        for v in vs:
+            if isinstance(v, tuple):
+                out += [v[1][:3], v[2][:3]] if v[0] == "ind" else [v[:3]]
+        return out
+
+    def rec(qn, call, r, w, sem=None, val=0, after=()):
+        ops.append({"q": qn, "call": call, "r": spans(r), "w": spans(w), "sem": sem, "ev": (sem, val),
+                    "after": list(after), "need": False})
+        return len(ops) - 1
+
+    def cp(o, i):
+        rec("v", lambda: g.vector.tensor_copy(ap(o), ap(i)), [i], [o])
+
+    def tt(o, a, b, op):
+        rec("v", lambda: g.vector.tensor_tensor(ap(o), ap(a), ap(b), op), [a, b], [o])
+
+    def ts(o, a, s1, op0, s2=None, op1=None):
+        if op1 is None:
+            rec("v", lambda: g.vector.tensor_scalar(ap(o), ap(a), ap(s1), None, op0), [a, s1], [o])
+        else:
+            rec("v", lambda: g.vector.tensor_scalar(ap(o), ap(a), ap(s1), ap(s2), op0, op1), [a, s1, s2], [o])
+
+    def scan(o, a, b, op0, op1):
+        rec("v", lambda: g.vector.tensor_tensor_scan(ap(o), ap(a), ap(b), 0.0, op0, op1), [a, b], [o])
+
+    def fill(o, c):
+        rec("v", lambda: g.vector.memset(ap(o), c), [], [o])
+
+    def turn(o, i):
+        rec("v", lambda: g.vector.transpose(ap(o), ap(i)), [i], [o])
+
+    def act(o, i, f, bias=0.0, scale=1.0):
+        rec("a", lambda: g.scalar.activation(ap(o), ap(i), f, bias=ap(bias), scale=scale), [i, bias], [o])
+
+    def mm(o, l, r, start, stop):
+        rec("p", lambda: g.tensor.matmul(ap(o), ap(l), ap(r), start, stop), [l, r], [o])
+
+    def load(qn, o, src, sem, after=()):
+        e = g.sync if qn == "s" else g.scalar
+        return rec(qn, lambda: e.dma_start(ap(o), src).then_inc(T.sem[sem], 16), [], [o], sem, 16, after)
+
+    def store(qn, dst, i, sem):
+        e = g.sync if qn == "s" else g.scalar
+        return rec(qn, lambda: e.dma_start(dst, ap(i)).then_inc(T.sem[sem], 16), [i], [], sem, 16)
+
+    sent = [0]
+
+    def send(p, after=()):
+        here, there = _sides(T, p, q)
+
+        def caller(hops):
+            return lambda: g.remote_dma_fused([RemoteDMATransfer(
+                dst_ids=[_dst(topo, d, core) for d in ds], dma_engine_mask=_bits(e), remote_sem=T.sem[s],
+                srcs=[here], dsts=[here if s[0] == "h" else there for d in ds]) for ds, e, s in hops],
+                local_sem=T.sem.sent)
+        for hops in _first_hop(T, topo, q, p):
+            sent[0] += sum(len(e) for d, e, s in hops)
+            rec("g", caller(hops), [vw("dx") if p == "x0" else vw(*_block(p, q))], [], "sent", -1, after)
+        rec(None, None, [], [vw(*_block(p, s)) for s in range(NR) if s != q], "a" + p, _arrivals(T, topo, q, p))
+
+    own = q * V
+    load("s", vw("dx"), T.x0[:], "ld")
+    load("a", vw("ei"), T.sc0[:], "le")
+    load("s", vw("ca"), T.cas[:], "lc")
+    load("a", vw("ti"), T.th[:], "lt")
+    load("a", vw("ro"), T.rol[:], "lr")
+    load("s", vw("xt", own, own + V), T.x0[:], "lx")
+    rec("g", lambda: g.iota(ap(vw("pi", 0, 1)), [[1, 1]], 0, 1), [], [vw("pi", 0, 1)])
+    rec("g", lambda: g.iota(ap(vw("col")), [[1, 144]], 0, 0), [], [vw("col")])
+    send("x0")
+    go = rec("g", lambda: g.sem_inc(T.sem.go, 1), [], [], "go", 1)
+    frl = load("s", vw("fr", 0, FCUT), T.frm[:, 0:FCUT], "lf1", [go])
+    load("s", vw("fr", FCUT, 4096), T.frm[:, FCUT:4096], "lf2")
+
+    P = vw("pi", 0, 1)
+    ts(vw("pi", 1, 2), P, 15, OP.bitwise_and)
+    ts(vw("pi", 2, 3), P, 7, OP.bitwise_and)
+    ts(vw("pi", 3, 4), P, 3, OP.arith_shift_right, 1, OP.bitwise_and)
+    ts(vw("pi", 4, 5), P, 16, OP.bitwise_and)
+    ts(vw("pi", 5, 6), P, 112, OP.bitwise_and)
+    ts(vw("u1", 0, 16), vw("col", 0, 16), 1, OP.arith_shift_right)
+    cp(vw("pf", 0, 6), vw("pi", 0, 6))
+    pP, pR, p7, p3, pG, pB = [vw("pf", i, i + 1) for i in range(6)]
+    ts(vw("pf", 8, 9), p7, 16.0, OP.mult, p3, OP.add)
+    ts(vw("pf", 9, 10), p7, 32.0, OP.mult, p3, OP.add)
+    ts(vw("pf", 10, 11), pR, 8.0, OP.mult)
+    ts(vw("pf", 11, 12), pR, pG, OP.add)
+    ts(vw("pf", 12, 13), pB, 15.0, OP.add)
+    c8 = vw("col", 0, 8)
+    ts(vw("lf", 0, 8), c8, 2.0, OP.mult, vw("pf", 8, 9), OP.add)
+    ts(vw("lf", 8, 16), c8, 2.0, OP.mult, vw("pf", 9, 10), OP.add)
+    ts(vw("lf", 16, 32), vw("u1", 0, 16), vw("pf", 10, 11), OP.add)
+    ts(vw("lf", 32, 40), c8, 32.0, OP.mult, vw("pf", 11, 12), OP.add)
+    cp(vw("lu"), vw("lf"))
+    PERM = vw("lu", 0, 8)
+    PERMD = vw("lu", 8, 16)
+    DUP = vw("lu", 16, 32)
+    SEL = vw("lu", 32, 40)
+
+    def frames_of(t):
+        src = vw("ei", t, 16, 2) if t < 2 else vw("en0")
+        cp(vw("sl", 16 * t, 16 * t + 16, 2), src)
+        cp(vw("sl", 16 * t + 1, 16 * t + 16, 2), src)
+        cp(vw("xf"), ind(vw("ro"), vw("sl", 16 * t, 16 * t + 16)))
+        cp(vw("ofr", H * (t % 2), H * (t % 2) + H), ind(vw("xf"), PERMD))
+
+    def frames_gather(t, lo, hi, on_vector=False):
+        o, i = vw("yg", 16 * lo, 16 * hi), ind(vw("fr"), vw("ofr", H * (t % 2) + lo, H * (t % 2) + hi))
+        if on_vector:
+            cp(o, i)
+        else:
+            act(o, i, AF.Copy)
+
+    def state(name, t):
+        return vw(name, own + t, own + V, 2) if t < 2 else vw(name, UE + q * H, UE + q * H + H)
+
+    def move(o, i, on_scalar):
+        if on_scalar:
+            act(o, i, AF.Copy)
+        else:
+            cp(o, i)
+
+    def cast_rows(t):
+        if t == 0:
+            cp(vw("cp"), vw("ca", 0, V, 2))
+        elif t == 1:
+            n = vw("ca", 1, V, 2)
+            ts(vw("u1"), n, 1, OP.bitwise_and)
+            ts(vw("u4"), n, 0.5, OP.mult, float(UE), OP.add)
+            ts(vw("u3"), vw("u1"), -4096.0, OP.mult, 4096.0, OP.add)
+            tt(vw("u5"), vw("u3"), n, OP.add)
+            tt(vw("cp"), vw("u5"), vw("u4"), OP.min)
+        else:
+            n = state("ct", 2)
+            cp(vw("u1"), n)
+            ts(vw("u4"), n, 1024.0, OP.mult)
+            ts(vw("u2"), vw("u1"), 1, OP.arith_shift_right)
+            ts(vw("u3"), vw("u2"), -2047.0, OP.mult)
+            tt(vw("cp"), vw("u3"), vw("u4"), OP.add)
+        move(vw("xc"), ind(vw("cp"), DUP), t < 2)
+        cp(vw("oxt", H * (t % 2), H * (t % 2) + H), vw("cp"))
+
+    def cast_turn(t):
+        b = 264 * (t % 2)
+        turn(vw("tc"), vw("xc"))
+        move(vw("pw", b + 136, b + 264), ind(vw("tc"), SEL), t < 2)
+
+    def frame_turn(t):
+        b = 264 * (t % 2)
+        turn(vw("tf"), vw("xf"))
+        move(vw("pw", b + 8, b + 136), ind(vw("tf"), SEL), t < 1)
+
+    def steps(t):
+        b = 264 * (t % 2)
+        tt(vw("dl", 256 * (t % 2), 256 * (t % 2) + 256), vw("pw", b + 7, b + 263), vw("pw", b + 8, b + 264), OP.subtract)
+
+    def halves(t):
+        act(vw("xoh"), state("xt", t), AF.Copy, scale=0.5)
+        act(vw("xoq"), state("xt", t), AF.Identity, bias=-0.25, scale=0.5)
+
+    def weights():
+        c128 = vw("col", 0, 128)
+        ts(vw("b16", 0, 144), vw("col"), vw("pf", 12, 13), OP.is_equal, KW, OP.mult)
+        ts(vw("ki"), c128, 15, OP.bitwise_and)
+        ts(vw("cg"), c128, 112, OP.bitwise_and)
+        fill(vw("ones"), 1.0)
+        ts(vw("kp"), c128, 1.0 / 128, OP.mult)
+        cp(vw("kb"), vw("ki"))
+        ts(vw("rst"), vw("ki"), 0.0, OP.is_equal, 8192 * KW, OP.mult)
+        ts(vw("gpw"), vw("cg"), pB, OP.is_equal, 256.0, OP.mult)
+        act(vw("gmw"), vw("gpw"), AF.Copy, scale=-1.0)
+        act(vw("t2"), vw("gpw"), AF.Copy, scale=16.0)
+        ts(vw("t1"), c128, pP, OP.is_equal, 131072.0, OP.mult)
+        fill(vw("cst", 0, 128), -10.0)
+        fill(vw("cst", 128, 256), -864.0)
+        act(vw("cst", 256, 512), vw("cst", 0, 256), AF.Copy, scale=-1.0)
+        tt(vw("vpw"), vw("t1"), vw("t2"), OP.subtract)
+        act(vw("vmw"), vw("vpw"), AF.Copy, scale=-1.0)
+
+    def pick(k):
+        return vw("b16", 15 - k, 143 - k)
+
+    def distances(t):
+        win = vw("xt", WIN[t][0], WIN[t][1])
+        mm(vw("key", 0, H), vw("ones"), vw("kp"), True, False)
+        mm(vw("key", 0, H), vw("kb"), vw("ones"), False, False)
+        for i, n in enumerate(("gp", "vp", "gm", "vm")):
+            mm(vw(n, 0, H), vw("ones"), vw("cst", 128 * i, 128 * i + 128), True, False)
+        for lo, hi in CHUNKS:
+            tt(vw("df", 16 * lo, 16 * hi), ind(win, vw("oxt", H * (t % 2) + lo, H * (t % 2) + hi)),
+               vw("yg", 16 * lo, 16 * hi), OP.subtract)
+            act(vw("ad", 16 * lo, 16 * hi), vw("df", 16 * lo, 16 * hi), AF.Abs)
+            for r in range(lo // 8, hi // 8):
+                mm(vw("key", 0, H), pick(r), vw("ad", 128 * r, 128 * r + 128), False, r == 15)
+            for a, k0, k1 in ROLES.get(hi, []):
+                for k in range(k0, k1):
+                    mm(vw("dr", a, a + 64), pick(k), vw("ad", 16 * a + k, 16 * a + 1024, 16), k == 0, k == 15)
+
+    def signs(t):
+        act(vw("sg"), vw("dr", 0, H), AF.Sign, bias=vw("bias", t, t + 1), scale=1.0 / KW)
+        for n in ("gm", "gp", "vp", "vm"):
+            mm(vw(n, 0, H), vw(n + "w"), vw("sg"), False, True)
+        for r in range(16):
+            mm(vw("jw", 0, 8), pick(r), vw("sg", 8 * r, 8 * r + 8), r == 0, r == 15)
+
+    def best(t, i, offsets=True):
+        lo, d, b = 128 * i, 256 * (t % 2) + 128 * i, 264 * (t % 2) + 128 * i
+        scan(vw("zz", lo, lo + 128), vw("dl", d, d + 128), vw("nn"), OP.add, OP.mult)
+        tt(vw("bi", 8 * i, 8 * i + 8), vw("zz", lo + 15, lo + 128, 16), vw("pw", b + 23, b + 136, 16), OP.add)
+        if offsets:
+            cp(vw("bu", 8 * i, 8 * i + 8), vw("bi", 8 * i, 8 * i + 8))
+
+    def cast_gather(t, on_scalar):
+        move(vw("ccj"), ind(vw("ct", WIN[t][0], WIN[t][1]), vw("bu", 8, 16)), on_scalar)
+
+    def features(t, out):
+        gp, gm = vw("gp", 0, H), vw("gm", 0, H)
+        scan(vw("mn"), vw("rst"), vw("key", 0, H), OP.add, OP.min)
+        if t < 2:
+            cp(vw("mi", 0, 8), vw("mn", 15, 128, 16))
+            tt(vw("nn"), vw("mn"), vw("key", 0, H), OP.not_equal)
+            ts(vw("mi", 8, 16), vw("mi", 0, 8), 2047, OP.bitwise_and)
+            cp(vw("bu", 16, 24), vw("mi", 8, 16))
+            act(vw("ybj"), ind(vw("yg"), vw("bu", 16, 24)), AF.Copy, scale=0.5)
+        else:
+            tt(vw("nn"), vw("mn"), vw("key", 0, H), OP.not_equal)
+            best(t, 0)
+            act(vw("ybj"), ind(vw("fr"), vw("bu", 0, 8)), AF.Copy, scale=0.5)
+        signs(t)
+        best(t, 1)
+        tt(vw("ddh"), ind(vw("ybj"), PERM), vw("xoh"), OP.subtract)
+        act(vw("aa"), vw("ddh"), AF.Abs, scale=2.0)
+        act(vw("vps"), vw("vp", 0, H), AF.Copy)
+        if t == 2:
+            cast_gather(t, True)
+        tt(vw("hh"), ind(vw("ybj"), PERM), vw("xoq"), OP.add)
+        return [lambda: tt(vw("p2"), vw("aa"), gm, OP.min),
+                lambda: tt(gp, vw("hh"), gp, OP.min),
+                lambda: tt(out, vw("p2"), gp, OP.max)]
+
+    def casts(t, out):
+        vm = vw("vm", 0, H)
+        return ([lambda: tt(vm, state("ct", t), vm, OP.min)] + ([lambda: cast_gather(t, False)] if t < 2 else [])
+                + [lambda: tt(vw("q1"), ind(vw("ccj"), PERM), vw("vps"), OP.min),
+                   lambda: tt(out, vw("q1"), vm, OP.max)])
+
+    def scenes(t, out):
+        nxt = vw("e1", t, 16, 2) if t < 2 else vw("e1", 40, 48)
+
+        def low():
+            if t < 2:
+                best(t, 0, False)
+            ts(vw("fm"), vw("bi", 0, 8), 1023, OP.bitwise_and)
+
+        def flag():
+            ts(vw("j01"), vw("jw", 0, 8), 5 * KW, OP.is_gt)
+            if t < 2:
+                mm(vw("at", 0, 8), vw("ones"), vw("j01"), True, True)
+        return [low, flag,
+                lambda: tt(vw("ed", 0, 8), vw("fm"), nxt, OP.subtract),
+                lambda: tt(vw("ed", 8, 16), vw("ed", 0, 8), vw("j01"), OP.mult),
+                lambda: tt(out, vw("ed", 8, 16), nxt, OP.add)]
+
+    def run(calls):
+        for c in calls:
+            c()
+
+    def weave(first, second):
+        runs = []
+        for calls in (first, second):
+            n = len(ops)
+            run(calls)
+            runs.append(ops[n:])
+            del ops[n:]
+        for i in range(max(len(r) for r in runs)):
+            for r in runs:
+                ops.extend(r[i:i + 1])
+
+    def jumps(t):
+        rec("v", lambda: g.vector.tensor_reduce(ap(vw("as1")), ap(vw("at", 0, 8)), AxisListType.X, OP.add),
+            [vw("at", 0, 8)], [vw("as1")])
+        cp(vw("ai", 0, 1), vw("as1"))
+        ts(vw("ai", 1, 2), vw("ai", 0, 1), 127, OP.bitwise_and)
+        ts(vw("bias", t + 1, t + 2), vw("ai", 1, 2), -1.0, OP.mult, vw("bias", 0, 1), OP.add)
+
+    fill(vw("pw", 0, 8), 0.0)
+    fill(vw("pw", 264, 272), 0.0)
+    weights()
+    ts(vw("e1", 16, 32), vw("ei"), 1.0, OP.add)
+    ts(vw("bias", 0, 1), vw("ti"), -1.0, OP.mult, -0.5, OP.add)
+    ts(vw("e1", 0, 16), vw("e1", 16, 32), 1023, OP.bitwise_and)
+    cast_rows(0)
+    cp(vw("cu", own, own + V), vw("ca"))
+    send("c0", [frl])
+    cast_turn(0)
+    frames_of(0)
+    frame_turn(0)
+    halves(0)
+    cast_rows(1)
+    steps(0)
+    cast_turn(1)
+    frames_of(1)
+    frame_turn(1)
+    steps(1)
+    frames_gather(0, 0, YV, True)
+    for lo, hi in ((YV, 64), (64, 88), (88, 104), (104, 128)):
+        frames_gather(0, lo, hi)
+
+    distances(0)
+    run(features(0, vw(*_block("x1", q))))
+    send("x1")
+    frames_gather(1, 0, H)
+    halves(1)
+    weave([lambda: run(scenes(0, vw("en0"))), lambda: jumps(0)],
+          [lambda: [cp(vw("ct", c, c + V), vw("cu", c, c + V)) for c in range(0, NR * V, V)]])
+    weave([lambda: run(casts(0, vw(*_block("c1", q)))), lambda: send("c1")],
+          [lambda: ts(vw("e1", 32, 40), vw("en0"), 1.0, OP.add), lambda: frames_of(2),
+           lambda: ts(vw("e1", 40, 48), vw("e1", 32, 40), 1023, OP.bitwise_and)])
+
+    distances(1)
+    run(features(1, vw(*_block("x2", q))))
+    send("x2")
+    frames_gather(2, 0, H)
+    halves(2)
+    weave([lambda: run(scenes(1, vw("oute", 1, 16, 2))), lambda: jumps(1)],
+          [lambda: run(casts(1, vw(*_block("c2", q)))), lambda: send("c2"), lambda: cast_rows(2)])
+    weave([lambda: frame_turn(2)], [lambda: cast_turn(2)])
+    steps(2)
+    act(vw("outx", 1, V, 2), vw(*_block("x2", q)), AF.Copy)
+    act(vw("outc", 1, V, 2), vw(*_block("c2", q)), AF.Copy)
+
+    distances(2)
+    fx = features(2, vw("outx", 0, V, 2))
+    fc, fe = casts(2, vw("outc", 0, V, 2)), scenes(2, vw("oute", 0, 16, 2))
+    run([fx[0], fx[1], fe[0], fx[2]])
+    s1 = store("s", T.yx[:], vw("outx"), "ox")
+    run([fe[2], fc[0], fe[1], fc[1], fe[3], fc[2]])
+    s2 = store("a", T.yc[:], vw("outc"), "oc")
+    run([fe[4]])
+    s3 = store("s", T.ye[:], vw("oute"), "oe")
+    rec("s", lambda: None, [], [], "end", 0, [s1, s2, s3])
+    _emit(ops, g, T)
+    g.wait_ge(T.sem.sent, sent[0])

@@ -4,11 +4,15 @@ from concourse.mybir import AluOpType as OP, AxisListType, ActivationFunctionTyp
 NR, V, H = 8, 256, 128
 UE, UO = 2048, 3072
 WIN = [(0, 2048), (0, 3072), (2048, 4096)]
-CHUNKS = [(0, 16), (16, 40), (40, 64), (64, 88), (88, 104), (104, 120), (120, 128)]
-YV = 40
+SA = 24
+CHUNKS = [(24, 48), (48, 72), (72, 96), (96, 112), (112, 120), (120, 128)]
+YV = 32
 FCUT = 3072
-ROLES = {64: [(0, 0, 6)], 88: [(0, 6, 10)], 104: [(0, 10, 12)], 128: [(0, 12, 16), (64, 0, 16)]}
-X0 = 0
+ROLES = {72: [(0, 0, 10)], 96: [(0, 10, 14)], 112: [(0, 14, 16)], 128: [(64, 0, 16)]}
+HX0, HX, HC, HC2 = (2, 3, 2), (2, 0, 0), (2, 0, 0), (2, 0, 0)
+HANDS = {"x0": HX0, "x1": HX, "x2": HX, "c0": HC, "c1": HC, "c2": HC2}
+F0 = 1024
+LATE = ()
 KW = 2048.0
 
 F, B, I, U = "float32", "bfloat16", "int32", "uint16"
@@ -19,17 +23,17 @@ def _sb(n, d):
 
 
 SCRATCH = {
-    "dx": ("dram", [128, 256], B), "cu": _sb(2048, U),
+    "dx": ("dram", [128, 256], B),
     "xt": _sb(4096, B), "ct": _sb(4096, F), "fr": _sb(4096, B), "ro": _sb(1024, I), "ca": _sb(256, I),
     "ei": _sb(16, I), "ti": _sb(1, I),
     "yg": _sb(2048, B), "df": _sb(2048, B), "ad": _sb(2048, B),
-    "col": _sb(144, I), "pi": _sb(8, I), "pf": _sb(16, F), "lf": _sb(40, F), "lu": _sb(40, U),
+    "col": _sb(24, I), "pi": _sb(8, I), "pf": _sb(16, F), "lu": _sb(40, U),
     "b16": _sb(144, B), "gpw": _sb(128, B), "gmw": _sb(128, B), "vpw": _sb(128, B), "vmw": _sb(128, B),
-    "ones": _sb(128, B), "kp": _sb(128, B), "kb": _sb(128, B), "cst": _sb(512, B), "rst": _sb(128, B),
-    "ki": _sb(128, I), "cg": _sb(128, I), "t1": _sb(128, F), "t2": _sb(128, F),
+    "ones": _sb(128, B), "eye": _sb(256, B), "xg": _sb(512, B), "kp": _sb(128, B), "kb": _sb(128, B), "cst": _sb(512, B), "rst": _sb(128, B),
+    "cf": _sb(144, F), "t1": _sb(144, F), "t2": _sb(128, F),
     "sl": _sb(48, U), "e1": _sb(48, I), "en0": _sb(8, F), "bias": _sb(4, F),
-    "ofr": _sb(256, U), "oxt": _sb(256, U), "cp": _sb(128, F),
-    "xf": _sb(256, F), "xc": _sb(256, F), "tf": _sb(256, F), "tc": _sb(256, F), "pw": _sb(528, F), "dl": _sb(512, F),
+    "ofr": _sb(256, U), "oxt": _sb(256, U), "cp": _sb(256, F),
+    "xf": _sb(256, F), "xc": _sb(512, F), "tf": _sb(256, F), "tc": _sb(256, F), "pw": _sb(528, F), "dl": _sb(512, F),
     "u1": _sb(128, I), "u2": _sb(128, I), "u3": _sb(128, F), "u4": _sb(128, F), "u5": _sb(128, F),
     "xoh": _sb(128, B), "xoq": _sb(128, F),
     "mn": _sb(128, F), "nn": _sb(128, F), "zz": _sb(256, F), "bi": _sb(16, I), "bu": _sb(24, U), "mi": _sb(16, I),
@@ -39,10 +43,10 @@ SCRATCH = {
     "outx": _sb(256, B), "outc": _sb(256, F), "oute": _sb(16, F),
     "key": ("psum", [128, 512], F), "dr": ("psum", [128, 512], F), "gp": ("psum", [128, 512], F),
     "gm": ("psum", [128, 512], F), "vp": ("psum", [128, 512], F), "vm": ("psum", [128, 512], F),
-    "jw": ("psum", [128, 512], F), "at": ("psum", [128, 512], F),
+    "jw": ("psum", [128, 512], F), "dp": ("psum", [128, 512], F),
 }
 PHASES = ["x0", "c0", "x1", "c1", "x2", "c2"]
-SEMAPHORES = (["qv", "qa", "qp", "qg", "go", "sent", "lx", "lc", "le", "lt", "lr", "ld", "lf1", "lf2", "ox", "oc", "oe"]
+SEMAPHORES = (["qv", "qa", "qp", "qg", "go", "sent", "lx", "lc", "le", "lt", "lr", "ld", "lf0", "lf1", "lf2", "ox", "oc", "oe"]
               + ["a" + p for p in PHASES] + ["h" + p for p in PHASES])
 PSUM = [n for n in SCRATCH if SCRATCH[n][0] == "psum"]
 COUNTER = {"v": "qv", "a": "qa", "p": "qp", "g": "qg"}
@@ -52,7 +56,7 @@ def _block(phase, q):
     name = "xt" if phase[0] == "x" else "ct"
     t = int(phase[1])
     if t == 0:
-        return "xt" if phase[0] == "x" else "cu", q * V, q * V + V
+        return name, q * V, q * V + V
     base = UE if t == 1 else UO
     return name, base + q * H, base + q * H + H
 
@@ -74,20 +78,16 @@ def _plan(T, topo, q):
     free = [c for c in topo.cores_of(me) if T.rank_of(c) is None]
     able = [c for c in free if all(topo.may_write(c, d) for d in far)]
     able.sort(key=lambda c: topo.die(c) == topo.die(me))
-    hf = able[:2]
-    rest = [c for c in free if c not in hf]
-    rest.sort(key=lambda c: topo.die(c) != topo.die(me))
-    hn = rest[:2]
+    rest = [c for c in free if c not in able]
+    rest.sort(key=lambda c: topo.die(c) == topo.die(me))
     plan = {}
     for p in PHASES:
-        relays = [(hf[0], far[0::2]), (hf[1], far[1::2])]
-        direct = near
-        if p == "x0" and X0 == 0:
-            relays = relays + [(hn[0], near[0::2]), (hn[1], near[1::2])]
-            direct = []
-        if p == "x0" and X0 == 1:
-            relays = [(able[i], [far[i]]) for i in range(len(far))]
-        plan[p] = (direct, relays)
+        nf, nn, rn = HANDS[p]
+        relays = [(able[i], far[i::nf]) for i in range(nf)]
+        pool = [rest[-1], able[2]]
+        relays += [(pool[i], near[len(near) - nn:][i::rn]) for i in range(rn)]
+        relays.sort(key=lambda r: -len(r[1]))
+        plan[p] = (near[:len(near) - nn], relays)
     return plan
 
 
@@ -106,7 +106,8 @@ def _first_hop(T, topo, q, p):
     off = topo.engines(me, direct[0])
     if p[0] == "x":
         return [[(hands, on, "h" + p)], [(direct, off, "a" + p)]]
-    return [[(direct, off, "a" + p), (hands, [e for e in on if e not in off], "h" + p)]]
+    hops = [(hands, [e for e in on if e not in off], "h" + p), (direct, off, "a" + p)]
+    return [hops]
 
 
 def _arrivals(T, topo, q, p):
@@ -264,20 +265,31 @@ def rank_program(g, core, T, topo):
         e = g.sync if qn == "s" else g.scalar
         return rec(qn, lambda: e.dma_start(dst, ap(i)).then_inc(T.sem[sem], 16), [i], [], sem, 16)
 
-    sent = [0]
+    sent, came = [0], {}
 
     def send(p, after=()):
         here, there = _sides(T, p, q)
 
-        def caller(hops):
-            return lambda: g.remote_dma_fused([RemoteDMATransfer(
-                dst_ids=[_dst(topo, d, core) for d in ds], dma_engine_mask=_bits(e), remote_sem=T.sem[s],
-                srcs=[here], dsts=[here if s[0] == "h" else there for d in ds]) for ds, e, s in hops],
-                local_sem=T.sem.sent)
+        def caller(hops, before):
+            def call():
+                if p[0] == "c" and hops[0][2][0] == "a":
+                    g.wait_ge(T.sem.sent, before)
+                return g.remote_dma_fused([RemoteDMATransfer(
+                    dst_ids=[_dst(topo, d, core) for d in ds], dma_engine_mask=_bits(e), remote_sem=T.sem[s],
+                    srcs=[here], dsts=[here if s[0] == "h" else there for d in ds]) for ds, e, s in hops],
+                    local_sem=T.sem.sent)
+            return call
+        go = None
+        if p in LATE:
+            after = list(after) + [came["x" + p[1]]]
         for hops in _first_hop(T, topo, q, p):
+            before = sent[0]
             sent[0] += sum(len(e) for d, e, s in hops)
-            rec("g", caller(hops), [vw("dx") if p == "x0" else vw(*_block(p, q))], [], "sent", -1, after)
-        rec(None, None, [], [vw(*_block(p, s)) for s in range(NR) if s != q], "a" + p, _arrivals(T, topo, q, p))
+            rec("g", caller(hops, before), [vw("dx") if p == "x0" else vw(*_block(p, q))], [], "sent", -1, after)
+            if p == "x0" and go is None:
+                go = rec("g", lambda: g.sem_inc(T.sem.go, 1), [], [], "go", 1)
+        came[p] = rec(None, None, [], [vw(*_block(p, s)) for s in range(NR) if s != q], "a" + p, _arrivals(T, topo, q, p))
+        return go
 
     own = q * V
     load("s", vw("dx"), T.x0[:], "ld")
@@ -285,13 +297,13 @@ def rank_program(g, core, T, topo):
     load("s", vw("ca"), T.cas[:], "lc")
     load("a", vw("ti"), T.th[:], "lt")
     load("a", vw("ro"), T.rol[:], "lr")
-    load("s", vw("xt", own, own + V), T.x0[:], "lx")
+    load("s", vw("fr", 0, F0), T.frm[:, 0:F0], "lf0")
     rec("g", lambda: g.iota(ap(vw("pi", 0, 1)), [[1, 1]], 0, 1), [], [vw("pi", 0, 1)])
-    rec("g", lambda: g.iota(ap(vw("col")), [[1, 144]], 0, 0), [], [vw("col")])
-    send("x0")
-    go = rec("g", lambda: g.sem_inc(T.sem.go, 1), [], [], "go", 1)
-    frl = load("s", vw("fr", 0, FCUT), T.frm[:, 0:FCUT], "lf1", [go])
-    load("s", vw("fr", FCUT, 4096), T.frm[:, FCUT:4096], "lf2")
+    rec("g", lambda: g.iota(ap(vw("col", 0, 8)), [[1, 8]], 0, 0), [], [vw("col", 0, 8)])
+    rec("g", lambda: g.iota(ap(vw("col", 8, 24)), [[1, 8], [0, 2]], 0, 0), [], [vw("col", 8, 24)])
+    rec("g", lambda: g.iota(ap(vw("cf")), [[1, 144]], 0, 0, allow_small_or_imprecise_dtypes=True), [], [vw("cf")])
+    go = send("x0")
+    rec("g", lambda: g.iota(ap(vw("kb")), [[0, 8], [1, 16]], 0, 0, allow_small_or_imprecise_dtypes=True), [], [vw("kb")])
 
     P = vw("pi", 0, 1)
     ts(vw("pi", 1, 2), P, 15, OP.bitwise_and)
@@ -299,29 +311,30 @@ def rank_program(g, core, T, topo):
     ts(vw("pi", 3, 4), P, 3, OP.arith_shift_right, 1, OP.bitwise_and)
     ts(vw("pi", 4, 5), P, 16, OP.bitwise_and)
     ts(vw("pi", 5, 6), P, 112, OP.bitwise_and)
-    ts(vw("u1", 0, 16), vw("col", 0, 16), 1, OP.arith_shift_right)
     cp(vw("pf", 0, 6), vw("pi", 0, 6))
     pP, pR, p7, p3, pG, pB = [vw("pf", i, i + 1) for i in range(6)]
     ts(vw("pf", 8, 9), p7, 16.0, OP.mult, p3, OP.add)
     ts(vw("pf", 9, 10), p7, 32.0, OP.mult, p3, OP.add)
     ts(vw("pf", 10, 11), pR, 8.0, OP.mult)
     ts(vw("pf", 11, 12), pR, pG, OP.add)
-    ts(vw("pf", 12, 13), pB, 15.0, OP.add)
+    act(vw("pf", 12, 13), pB, AF.Identity, bias=15.0)
+    act(vw("pf", 13, 14), pB, AF.Identity, bias=7.5)
     c8 = vw("col", 0, 8)
-    ts(vw("lf", 0, 8), c8, 2.0, OP.mult, vw("pf", 8, 9), OP.add)
-    ts(vw("lf", 8, 16), c8, 2.0, OP.mult, vw("pf", 9, 10), OP.add)
-    ts(vw("lf", 16, 32), vw("u1", 0, 16), vw("pf", 10, 11), OP.add)
-    ts(vw("lf", 32, 40), c8, 32.0, OP.mult, vw("pf", 11, 12), OP.add)
-    cp(vw("lu"), vw("lf"))
+    ts(vw("lu", 16, 32), vw("col", 8, 24), vw("pf", 10, 11), OP.add)
+    ts(vw("lu", 32, 40), c8, 32.0, OP.mult, vw("pf", 11, 12), OP.add)
+    ts(vw("lu", 8, 16), c8, 2.0, OP.mult, vw("pf", 9, 10), OP.add)
+    ts(vw("lu", 0, 8), c8, 2.0, OP.mult, vw("pf", 8, 9), OP.add)
     PERM = vw("lu", 0, 8)
     PERMD = vw("lu", 8, 16)
     DUP = vw("lu", 16, 32)
     SEL = vw("lu", 32, 40)
 
-    def frames_of(t):
+    def scene_list(t):
         src = vw("ei", t, 16, 2) if t < 2 else vw("en0")
         cp(vw("sl", 16 * t, 16 * t + 16, 2), src)
         cp(vw("sl", 16 * t + 1, 16 * t + 16, 2), src)
+
+    def frames_of(t):
         cp(vw("xf"), ind(vw("ro"), vw("sl", 16 * t, 16 * t + 16)))
         cp(vw("ofr", H * (t % 2), H * (t % 2) + H), ind(vw("xf"), PERMD))
 
@@ -342,29 +355,29 @@ def rank_program(g, core, T, topo):
             cp(o, i)
 
     def cast_rows(t):
+        col = vw("cp", H * (t % 2), H * (t % 2) + H)
         if t == 0:
-            cp(vw("cp"), vw("ca", 0, V, 2))
+            cp(col, vw("ca", 0, V, 2))
         elif t == 1:
             n = vw("ca", 1, V, 2)
             ts(vw("u1"), n, 1, OP.bitwise_and)
             ts(vw("u4"), n, 0.5, OP.mult, float(UE), OP.add)
             ts(vw("u3"), vw("u1"), -4096.0, OP.mult, 4096.0, OP.add)
             tt(vw("u5"), vw("u3"), n, OP.add)
-            tt(vw("cp"), vw("u5"), vw("u4"), OP.min)
+            tt(col, vw("u5"), vw("u4"), OP.min)
         else:
             n = state("ct", 2)
-            cp(vw("u1"), n)
+            ts(vw("u2"), n, 0.5, OP.mult, -0.25, OP.add)
             ts(vw("u4"), n, 1024.0, OP.mult)
-            ts(vw("u2"), vw("u1"), 1, OP.arith_shift_right)
             ts(vw("u3"), vw("u2"), -2047.0, OP.mult)
-            tt(vw("cp"), vw("u3"), vw("u4"), OP.add)
-        move(vw("xc"), ind(vw("cp"), DUP), t < 2)
-        cp(vw("oxt", H * (t % 2), H * (t % 2) + H), vw("cp"))
+            tt(col, vw("u3"), vw("u4"), OP.add)
+        move(vw("xc", V * (t % 2), V * (t % 2) + V), ind(col, DUP), t < 2)
+        cp(vw("oxt", H * (t % 2), H * (t % 2) + H), col)
 
     def cast_turn(t):
         b = 264 * (t % 2)
-        turn(vw("tc"), vw("xc"))
-        move(vw("pw", b + 136, b + 264), ind(vw("tc"), SEL), t < 2)
+        turn(vw("tc"), vw("xc", V * (t % 2), V * (t % 2) + V))
+        move(vw("pw", b + 136, b + 264), ind(vw("tc"), SEL), t < 1)
 
     def frame_turn(t):
         b = 264 * (t % 2)
@@ -380,22 +393,26 @@ def rank_program(g, core, T, topo):
         act(vw("xoq"), state("xt", t), AF.Identity, bias=-0.25, scale=0.5)
 
     def weights():
-        c128 = vw("col", 0, 128)
-        ts(vw("b16", 0, 144), vw("col"), vw("pf", 12, 13), OP.is_equal, KW, OP.mult)
-        ts(vw("ki"), c128, 15, OP.bitwise_and)
-        ts(vw("cg"), c128, 112, OP.bitwise_and)
-        fill(vw("ones"), 1.0)
-        ts(vw("kp"), c128, 1.0 / 128, OP.mult)
-        cp(vw("kb"), vw("ki"))
-        ts(vw("rst"), vw("ki"), 0.0, OP.is_equal, 8192 * KW, OP.mult)
-        ts(vw("gpw"), vw("cg"), pB, OP.is_equal, 256.0, OP.mult)
+        c128, t1, t2 = vw("cf", 0, 128), vw("t1", 0, 128), vw("t2")
+        act(vw("t1"), vw("cf"), AF.Abs, bias=vw("pf", 12, 13), scale=-1.0)
+        act(vw("b16"), vw("t1"), AF.Relu, bias=KW, scale=-KW)
+        act(t2, c128, AF.Abs, bias=pP, scale=-1.0)
+        act(vw("eye", 0, 128), t2, AF.Relu, bias=1.0, scale=-1.0)
+        act(vw("eye", 128, 256), vw("eye", 0, 128), AF.Copy, scale=-1.0)
+        act(t1, c128, AF.Abs, bias=vw("pf", 13, 14), scale=-1.0)
+        act(t2, t1, AF.Sign, bias=8.0, scale=-1.0)
+        act(vw("gpw"), t2, AF.Relu, scale=256.0)
         act(vw("gmw"), vw("gpw"), AF.Copy, scale=-1.0)
-        act(vw("t2"), vw("gpw"), AF.Copy, scale=16.0)
-        ts(vw("t1"), c128, pP, OP.is_equal, 131072.0, OP.mult)
+        act(t2, vw("gpw"), AF.Copy, scale=16.0)
+        act(t1, vw("eye", 0, 128), AF.Copy, scale=131072.0)
+        act(vw("kp"), c128, AF.Copy, scale=1.0 / 128)
+        fill(vw("ones"), 1.0)
         fill(vw("cst", 0, 128), -10.0)
         fill(vw("cst", 128, 256), -864.0)
         act(vw("cst", 256, 512), vw("cst", 0, 256), AF.Copy, scale=-1.0)
-        tt(vw("vpw"), vw("t1"), vw("t2"), OP.subtract)
+
+    def weights_end():
+        tt(vw("vpw"), vw("t1", 0, 128), vw("t2"), OP.subtract)
         act(vw("vmw"), vw("vpw"), AF.Copy, scale=-1.0)
 
     def pick(k):
@@ -407,29 +424,43 @@ def rank_program(g, core, T, topo):
         mm(vw("key", 0, H), vw("kb"), vw("ones"), False, False)
         for i, n in enumerate(("gp", "vp", "gm", "vm")):
             mm(vw(n, 0, H), vw("ones"), vw("cst", 128 * i, 128 * i + 128), True, False)
+        n = 16 * SA
+
+        def sums(lo, hi, src):
+            act(vw("ad", 16 * lo, 16 * hi), src, AF.Abs)
+            for r in range(lo // 8, hi // 8):
+                mm(vw("key", 0, H), pick(r), vw("ad", 128 * r, 128 * r + 128), False, r == 15)
+        mm(vw("dp", 0, n), vw("eye", 128, 256), vw("yg", 0, n), True, False)
+        act(vw("xg", 0, n), ind(win, vw("oxt", H * (t % 2), H * (t % 2) + SA)), AF.Copy)
+        mm(vw("dp", 0, n), vw("eye", 0, 128), vw("xg", 0, n), False, True)
         for lo, hi in CHUNKS:
             tt(vw("df", 16 * lo, 16 * hi), ind(win, vw("oxt", H * (t % 2) + lo, H * (t % 2) + hi)),
                vw("yg", 16 * lo, 16 * hi), OP.subtract)
-            act(vw("ad", 16 * lo, 16 * hi), vw("df", 16 * lo, 16 * hi), AF.Abs)
-            for r in range(lo // 8, hi // 8):
-                mm(vw("key", 0, H), pick(r), vw("ad", 128 * r, 128 * r + 128), False, r == 15)
+            sums(lo, hi, vw("df", 16 * lo, 16 * hi))
+            if lo == SA:
+                sums(0, SA, vw("dp", 0, n))
             for a, k0, k1 in ROLES.get(hi, []):
                 for k in range(k0, k1):
                     mm(vw("dr", a, a + 64), pick(k), vw("ad", 16 * a + k, 16 * a + 1024, 16), k == 0, k == 15)
 
     def signs(t):
         act(vw("sg"), vw("dr", 0, H), AF.Sign, bias=vw("bias", t, t + 1), scale=1.0 / KW)
-        for n in ("gm", "gp", "vp", "vm"):
-            mm(vw(n, 0, H), vw(n + "w"), vw("sg"), False, True)
-        for r in range(16):
-            mm(vw("jw", 0, 8), pick(r), vw("sg", 8 * r, 8 * r + 8), r == 0, r == 15)
+        order = ("gm", "gp", "vp", "vm", "jw") if t < 2 else ("vp", "vm", "jw", "gm", "gp")
+        for n in order:
+            if n != "jw":
+                mm(vw(n, 0, H), vw(n + "w"), vw("sg"), False, True)
+            else:
+                for r in range(16):
+                    mm(vw("jw", 0, 8), pick(r), vw("sg", 8 * r, 8 * r + 8), r == 0, r == 15)
 
-    def best(t, i, offsets=True):
-        lo, d, b = 128 * i, 256 * (t % 2) + 128 * i, 264 * (t % 2) + 128 * i
+    def carry(t, i):
+        lo, d = 128 * i, 256 * (t % 2) + 128 * i
         scan(vw("zz", lo, lo + 128), vw("dl", d, d + 128), vw("nn"), OP.add, OP.mult)
-        tt(vw("bi", 8 * i, 8 * i + 8), vw("zz", lo + 15, lo + 128, 16), vw("pw", b + 23, b + 136, 16), OP.add)
-        if offsets:
-            cp(vw("bu", 8 * i, 8 * i + 8), vw("bi", 8 * i, 8 * i + 8))
+
+    def best(t):
+        b = 264 * (t % 2)
+        tt(vw("bi"), vw("zz", 15, 256, 16), vw("pw", b + 23, b + 264, 16), OP.add)
+        cp(vw("bu", 0, 16), vw("bi"))
 
     def cast_gather(t, on_scalar):
         move(vw("ccj"), ind(vw("ct", WIN[t][0], WIN[t][1]), vw("bu", 8, 16)), on_scalar)
@@ -439,23 +470,30 @@ def rank_program(g, core, T, topo):
         scan(vw("mn"), vw("rst"), vw("key", 0, H), OP.add, OP.min)
         if t < 2:
             cp(vw("mi", 0, 8), vw("mn", 15, 128, 16))
-            tt(vw("nn"), vw("mn"), vw("key", 0, H), OP.not_equal)
             ts(vw("mi", 8, 16), vw("mi", 0, 8), 2047, OP.bitwise_and)
             cp(vw("bu", 16, 24), vw("mi", 8, 16))
             act(vw("ybj"), ind(vw("yg"), vw("bu", 16, 24)), AF.Copy, scale=0.5)
+            signs(t)
+            tt(vw("nn"), vw("mn"), vw("key", 0, H), OP.not_equal)
+            carry(t, 1)
         else:
             tt(vw("nn"), vw("mn"), vw("key", 0, H), OP.not_equal)
-            best(t, 0)
+            signs(t)
+            carry(t, 0)
+            carry(t, 1)
+            best(t)
+            act(vw("vps"), vw("vp", 0, H), AF.Copy)
             act(vw("ybj"), ind(vw("fr"), vw("bu", 0, 8)), AF.Copy, scale=0.5)
-        signs(t)
-        best(t, 1)
-        tt(vw("ddh"), ind(vw("ybj"), PERM), vw("xoh"), OP.subtract)
-        act(vw("aa"), vw("ddh"), AF.Abs, scale=2.0)
-        act(vw("vps"), vw("vp", 0, H), AF.Copy)
-        if t == 2:
             cast_gather(t, True)
-        tt(vw("hh"), ind(vw("ybj"), PERM), vw("xoq"), OP.add)
-        return [lambda: tt(vw("p2"), vw("aa"), gm, OP.min),
+
+        def differ():
+            tt(vw("ddh"), ind(vw("ybj"), PERM), vw("xoh"), OP.subtract)
+            act(vw("aa"), vw("ddh"), AF.Abs, scale=2.0)
+            if t < 2:
+                act(vw("vps"), vw("vp", 0, H), AF.Copy)
+        return [differ,
+                lambda: tt(vw("hh"), ind(vw("ybj"), PERM), vw("xoq"), OP.add),
+                lambda: tt(vw("p2"), vw("aa"), gm, OP.min),
                 lambda: tt(gp, vw("hh"), gp, OP.min),
                 lambda: tt(out, vw("p2"), gp, OP.max)]
 
@@ -470,13 +508,14 @@ def rank_program(g, core, T, topo):
 
         def low():
             if t < 2:
-                best(t, 0, False)
+                carry(t, 0)
+                best(t)
             ts(vw("fm"), vw("bi", 0, 8), 1023, OP.bitwise_and)
 
         def flag():
             ts(vw("j01"), vw("jw", 0, 8), 5 * KW, OP.is_gt)
             if t < 2:
-                mm(vw("at", 0, 8), vw("ones"), vw("j01"), True, True)
+                mm(vw("jw", 8, 16), vw("ones"), vw("j01"), True, True)
         return [low, flag,
                 lambda: tt(vw("ed", 0, 8), vw("fm"), nxt, OP.subtract),
                 lambda: tt(vw("ed", 8, 16), vw("ed", 0, 8), vw("j01"), OP.mult),
@@ -498,8 +537,8 @@ def rank_program(g, core, T, topo):
                 ops.extend(r[i:i + 1])
 
     def jumps(t):
-        rec("v", lambda: g.vector.tensor_reduce(ap(vw("as1")), ap(vw("at", 0, 8)), AxisListType.X, OP.add),
-            [vw("at", 0, 8)], [vw("as1")])
+        rec("v", lambda: g.vector.tensor_reduce(ap(vw("as1")), ap(vw("jw", 8, 16)), AxisListType.X, OP.add),
+            [vw("jw", 8, 16)], [vw("as1")])
         cp(vw("ai", 0, 1), vw("as1"))
         ts(vw("ai", 1, 2), vw("ai", 0, 1), 127, OP.bitwise_and)
         ts(vw("bias", t + 1, t + 2), vw("ai", 1, 2), -1.0, OP.mult, vw("bias", 0, 1), OP.add)
@@ -510,42 +549,52 @@ def rank_program(g, core, T, topo):
     ts(vw("e1", 16, 32), vw("ei"), 1.0, OP.add)
     ts(vw("bias", 0, 1), vw("ti"), -1.0, OP.mult, -0.5, OP.add)
     ts(vw("e1", 0, 16), vw("e1", 16, 32), 1023, OP.bitwise_and)
+    scene_list(0)
+    scene_list(1)
     cast_rows(0)
-    cp(vw("cu", own, own + V), vw("ca"))
-    send("c0", [frl])
+    cast_rows(1)
+    weights_end()
     cast_turn(0)
+    cp(vw("ct", own, own + V), vw("ca"))
+    load("s", vw("xt", own, own + V), T.x0[:], "lx", [go])
+    frl = load("s", vw("fr", F0, FCUT), T.frm[:, F0:FCUT], "lf1")
+    load("s", vw("fr", FCUT, 4096), T.frm[:, FCUT:4096], "lf2")
+    send("c0", [frl])
     frames_of(0)
     frame_turn(0)
-    halves(0)
-    cast_rows(1)
-    steps(0)
-    cast_turn(1)
     frames_of(1)
-    frame_turn(1)
-    steps(1)
+    steps(0)
+    act(vw("rst"), vw("kb"), AF.Relu, bias=8192 * KW, scale=-8192 * KW)
+    halves(0)
     frames_gather(0, 0, YV, True)
-    for lo, hi in ((YV, 64), (64, 88), (88, 104), (104, 128)):
+    for lo, hi in ((YV, 48), (48, 72), (72, 96), (96, H)):
         frames_gather(0, lo, hi)
 
     distances(0)
     run(features(0, vw(*_block("x1", q))))
     send("x1")
-    frames_gather(1, 0, H)
+    frames_gather(1, 0, YV)
+    frames_gather(1, YV, H)
     halves(1)
-    weave([lambda: run(scenes(0, vw("en0"))), lambda: jumps(0)],
-          [lambda: [cp(vw("ct", c, c + V), vw("cu", c, c + V)) for c in range(0, NR * V, V)]])
-    weave([lambda: run(casts(0, vw(*_block("c1", q)))), lambda: send("c1")],
-          [lambda: ts(vw("e1", 32, 40), vw("en0"), 1.0, OP.add), lambda: frames_of(2),
+    fe = scenes(0, vw("en0"))
+    run(fe[:1])
+    weave([lambda: run(casts(0, vw(*_block("c1", q)))), lambda: send("c1"), lambda: cast_turn(1), lambda: frame_turn(1)],
+          [lambda: run(fe[1:]), lambda: jumps(0), lambda: scene_list(2)])
+    weave([lambda: frames_of(2), lambda: steps(1)],
+          [lambda: ts(vw("e1", 32, 40), vw("en0"), 1.0, OP.add),
            lambda: ts(vw("e1", 40, 48), vw("e1", 32, 40), 1023, OP.bitwise_and)])
 
     distances(1)
     run(features(1, vw(*_block("x2", q))))
     send("x2")
-    frames_gather(2, 0, H)
+    frames_gather(2, 0, YV)
+    frames_gather(2, YV, H)
     halves(2)
-    weave([lambda: run(scenes(1, vw("oute", 1, 16, 2))), lambda: jumps(1)],
-          [lambda: run(casts(1, vw(*_block("c2", q)))), lambda: send("c2"), lambda: cast_rows(2)])
-    weave([lambda: frame_turn(2)], [lambda: cast_turn(2)])
+    fe = scenes(1, vw("oute", 1, 16, 2))
+    run(fe[:1])
+    weave([lambda: run(casts(1, vw(*_block("c2", q)))), lambda: send("c2"), lambda: cast_rows(2)],
+          [lambda: run(fe[1:]), lambda: jumps(1), lambda: frame_turn(2)])
+    cast_turn(2)
     steps(2)
     act(vw("outx", 1, V, 2), vw(*_block("x2", q)), AF.Copy)
     act(vw("outc", 1, V, 2), vw(*_block("c2", q)), AF.Copy)
@@ -553,12 +602,12 @@ def rank_program(g, core, T, topo):
     distances(2)
     fx = features(2, vw("outx", 0, V, 2))
     fc, fe = casts(2, vw("outc", 0, V, 2)), scenes(2, vw("oute", 0, 16, 2))
-    run([fx[0], fx[1], fe[0], fx[2]])
-    s1 = store("s", T.yx[:], vw("outx"), "ox")
-    run([fe[2], fc[0], fe[1], fc[1], fe[3], fc[2]])
+    run([fe[0], fc[0], fe[2], fx[0], fx[1], fe[1], fc[1], fe[3], fx[2], fe[4]])
+    s1 = store("s", T.ye[:], vw("oute"), "oe")
+    run([fc[2]])
     s2 = store("a", T.yc[:], vw("outc"), "oc")
-    run([fe[4]])
-    s3 = store("s", T.ye[:], vw("oute"), "oe")
+    run([fx[3], fx[4]])
+    s3 = store("s", T.yx[:], vw("outx"), "ox")
     rec("s", lambda: None, [], [], "end", 0, [s1, s2, s3])
     _emit(ops, g, T)
     g.wait_ge(T.sem.sent, sent[0])

from concourse.bass import DstId, RemoteDMATransfer
from concourse.mybir import AluOpType as OP, AxisListType, ActivationFunctionType as AF

NR, V, H = 8, 256, 128
UE, UO = 2048, 3072
WIN = [(0, 2048), (0, 3072), (2048, 4096)]
SA = 24
CHUNKS = [(24, 48), (48, 72), (72, 96), (96, 112), (112, 120), (120, 128)]
YV = 32
FCUT = 3072
ROLES = {72: [(0, 0, 10)], 96: [(0, 10, 14)], 112: [(0, 14, 16)], 128: [(64, 0, 16)]}
HX0, HX, HC, HC2 = (2, 3, 2), (2, 0, 0), (2, 0, 0), (2, 0, 0)
HANDS = {"x0": HX0, "x1": HX, "x2": HX, "c0": HC, "c1": HC, "c2": HC2}
F0 = 1024
LATE = ()
KW = 2048.0

F, B, I, U = "float32", "bfloat16", "int32", "uint16"


def _sb(n, d):
    return ("sbuf", [128, n], d)


SCRATCH = {
    "dx": ("dram", [128, 256], B),
    "xt": _sb(4096, B), "ct": _sb(4096, F), "fr": _sb(4096, B), "ro": _sb(1024, I), "ca": _sb(256, I),
    "ei": _sb(16, I), "ti": _sb(1, I),
    "yg": _sb(2048, B), "df": _sb(2048, B), "ad": _sb(2048, B),
    "col": _sb(24, I), "pi": _sb(8, I), "pf": _sb(16, F), "lu": _sb(40, U),
    "b16": _sb(144, B), "gpw": _sb(128, B), "gmw": _sb(128, B), "vpw": _sb(128, B), "vmw": _sb(128, B),
    "ones": _sb(128, B), "eye": _sb(256, B), "xg": _sb(512, B), "kp": _sb(128, B), "kb": _sb(128, B), "cst": _sb(512, B), "rst": _sb(128, B),
    "cf": _sb(144, F), "t1": _sb(144, F), "t2": _sb(128, F),
    "sl": _sb(48, U), "e1": _sb(48, I), "en0": _sb(8, F), "bias": _sb(4, F),
    "ofr": _sb(256, U), "oxt": _sb(256, U), "cp": _sb(256, F),
    "xf": _sb(256, F), "xc": _sb(512, F), "tf": _sb(256, F), "tc": _sb(256, F), "pw": _sb(528, F), "dl": _sb(512, F),
    "u1": _sb(128, I), "u2": _sb(128, I), "u3": _sb(128, F), "u4": _sb(128, F), "u5": _sb(128, F),
    "xoh": _sb(128, B), "xoq": _sb(128, F),
    "mn": _sb(128, F), "nn": _sb(128, F), "zz": _sb(256, F), "bi": _sb(16, I), "bu": _sb(24, U), "mi": _sb(16, I),
    "sg": _sb(128, B), "ybj": _sb(128, B), "ddh": _sb(128, B), "aa": _sb(128, B), "hh": _sb(128, I),
    "p2": _sb(128, B), "vps": _sb(128, F), "ccj": _sb(128, F), "q1": _sb(128, F),
    "j01": _sb(8, B), "fm": _sb(8, I), "ed": _sb(16, F), "as1": _sb(1, F), "ai": _sb(2, I),
    "outx": _sb(256, B), "outc": _sb(256, F), "oute": _sb(16, F),
    "key": ("psum", [128, 512], F), "dr": ("psum", [128, 512], F), "gp": ("psum", [128, 512], F),
    "gm": ("psum", [128, 512], F), "vp": ("psum", [128, 512], F), "vm": ("psum", [128, 512], F),
    "jw": ("psum", [128, 512], F), "dp": ("psum", [128, 512], F),
}
PHASES = ["x0", "c0", "x1", "c1", "x2", "c2"]
SEMAPHORES = (["qv", "qa", "qp", "qg", "go", "sent", "lx", "lc", "le", "lt", "lr", "ld", "lf0", "lf1", "lf2", "ox", "oc", "oe"]
              + ["a" + p for p in PHASES] + ["h" + p for p in PHASES])
PSUM = [n for n in SCRATCH if SCRATCH[n][0] == "psum"]
COUNTER = {"v": "qv", "a": "qa", "p": "qp", "g": "qg"}


def _block(phase, q):
    name = "xt" if phase[0] == "x" else "ct"
    t = int(phase[1])
    if t == 0:
        return name, q * V, q * V + V
    base = UE if t == 1 else UO
    return name, base + q * H, base + q * H + H


def _bits(engines):
    m = 0
    for e in engines:
        m |= 1 << e
    return m


def _plan(T, topo, q):
    me = T.cores[q]
    others = [T.cores[(q + d) % NR] for d in range(1, NR)]
    near = [c for c in others if topo.may_write(me, c)]
    far = [c for c in T.cores if c != me and not topo.may_write(me, c)]
    turn = len([c for c in near if T.rank_of(c) < q]) % len(far)
    far = far[turn:] + far[:turn]
    free = [c for c in topo.cores_of(me) if T.rank_of(c) is None]
    able = [c for c in free if all(topo.may_write(c, d) for d in far)]
    able.sort(key=lambda c: topo.die(c) == topo.die(me))
    rest = [c for c in free if c not in able]
    rest.sort(key=lambda c: topo.die(c) == topo.die(me))
    plan = {}
    for p in PHASES:
        nf, nn, rn = HANDS[p]
        relays = [(able[i], far[i::nf]) for i in range(nf)]
        pool = [rest[-1], able[2]]
        relays += [(pool[i], near[len(near) - nn:][i::rn]) for i in range(rn)]
        relays.sort(key=lambda r: -len(r[1]))
        plan[p] = (near[:len(near) - nn], relays)
    return plan


def _dst(topo, d, s):
    rid, pid = topo.addr(d, s)
    return DstId(rid=rid, pnc=pid)


def _first_hop(T, topo, q, p):
    me = T.cores[q]
    direct, relays = _plan(T, topo, q)[p]
    on = topo.engines(me, relays[0][0])
    hands = [h for h, d in relays]
    if not direct:
        return [[(hands, on, "h" + p)]]
    off = topo.engines(me, direct[0])
    if p[0] == "x":
        return [[(hands, on, "h" + p)], [(direct, off, "a" + p)]]
    hops = [(hands, [e for e in on if e not in off], "h" + p), (direct, off, "a" + p)]
    return [hops]


def _arrivals(T, topo, q, p):
    me, n = T.cores[q], 0
    for s in range(NR):
        if s == q:
            continue
        for call in _first_hop(T, topo, s, p):
            for dsts, eng, sem in call:
                if me in dsts:
                    n += len(eng)
        for h, dsts in _plan(T, topo, s)[p][1]:
            if me in dsts:
                n += len(topo.engines(h, me))
    return n


def _sides(T, p, q):
    name, lo, hi = _block(p, q)
    return (T.dx[:] if p == "x0" else T[name][:, lo:hi]), T[name][:, lo:hi]


def _relay(g, core, T, topo):
    own = [c for c in topo.cores_of(core) if T.rank_of(c) is not None]
    if not own:
        return
    q = T.rank_of(own[0])
    plan, sent = _plan(T, topo, q), 0
    for p in PHASES:
        for h, dsts in plan[p][1]:
            if h != core:
                continue
            got = [len(e) for call in _first_hop(T, topo, q, p) for d, e, s in call if core in d][0]
            here, there = _sides(T, p, q)
            eng = topo.engines(core, dsts[0])
            g.wait_ge(T.sem["h" + p], got)
            g.remote_dma_fused([RemoteDMATransfer(
                dst_ids=[_dst(topo, d, core) for d in dsts], dma_engine_mask=_bits(eng), remote_sem=T.sem["a" + p],
                srcs=[here], dsts=[there for d in dsts])], local_sem=T.sem.sent)
            sent += len(eng)
    if sent:
        g.wait_ge(T.sem.sent, sent)


def _emit(ops, g, T):
    queue = {"v": g.vector, "a": g.scalar, "p": g.tensor, "g": g, "s": g.sync}
    known = {k: {} for k in queue}
    seen = {}
    for n, o in enumerate(ops):
        deps = set(o["after"])
        for wr, views in ((False, o["r"]), (True, o["w"])):
            for name, lo, hi in views:
                for m, w2, l2, h2 in seen.get(name, []):
                    same = ops[m]["q"] == o["q"] and ops[m]["sem"] is None
                    if name in PSUM:
                        if not same or (o["q"] != "p" and (wr or w2)):
                            deps.add(m)
                    elif (wr or w2) and lo < h2 and l2 < hi:
                        deps.add(m)
        deps.discard(n)
        for wr, views in ((False, o["r"]), (True, o["w"])):
            for name, lo, hi in views:
                seen.setdefault(name, []).append((n, wr, lo, hi))
        o["src"] = o["sem"] if o["sem"] else o["q"]
        o["waits"] = []
        if o["q"] is None:
            o["clock"] = {o["src"]: n}
            continue
        k = known[o["q"]]
        for m in sorted(deps, reverse=True):
            if k.get(ops[m]["src"], -1) < m:
                o["waits"].append(m)
                ops[m]["need"] = True
                for s, x in ops[m]["clock"].items():
                    k[s] = max(k.get(s, -1), x)
        o["clock"] = dict(k)
        o["clock"][o["src"]] = n
    count = {k: 0 for k in COUNTER}
    for o in ops:
        if o["q"] is None:
            continue
        for m in o["waits"]:
            queue[o["q"]].wait_ge(T.sem[ops[m]["ev"][0]], ops[m]["ev"][1])
        ins = o["call"]()
        if o["sem"] is None and o["need"]:
            count[o["q"]] += 1
            ins.then_inc(T.sem[COUNTER[o["q"]]], 1)
            o["ev"] = (COUNTER[o["q"]], count[o["q"]])


def rank_program(g, core, T, topo):
    q = T.rank_of(core)
    if q is None:
        _relay(g, core, T, topo)
        return
    ops = []

    def vw(name, lo=0, hi=None, st=1):
        return (name, lo, SCRATCH[name][1][1] if hi is None else hi, st)

    def ind(win, off):
        return ("ind", win, off)

    def ap(v):
        if not isinstance(v, tuple):
            return v
        if v[0] == "ind":
            return ap(v[1]).indirect(ap(v[2]))
        return T[v[0]][:, v[1]:v[2]] if v[3] == 1 else T[v[0]][:, v[1]:v[2]:v[3]]

    def spans(vs):
        out = []
        for v in vs:
            if isinstance(v, tuple):
                out += [v[1][:3], v[2][:3]] if v[0] == "ind" else [v[:3]]
        return out

    def rec(qn, call, r, w, sem=None, val=0, after=()):
        ops.append({"q": qn, "call": call, "r": spans(r), "w": spans(w), "sem": sem, "ev": (sem, val),
                    "after": list(after), "need": False})
        return len(ops) - 1

    def cp(o, i):
        rec("v", lambda: g.vector.tensor_copy(ap(o), ap(i)), [i], [o])

    def tt(o, a, b, op):
        rec("v", lambda: g.vector.tensor_tensor(ap(o), ap(a), ap(b), op), [a, b], [o])

    def ts(o, a, s1, op0, s2=None, op1=None):
        if op1 is None:
            rec("v", lambda: g.vector.tensor_scalar(ap(o), ap(a), ap(s1), None, op0), [a, s1], [o])
        else:
            rec("v", lambda: g.vector.tensor_scalar(ap(o), ap(a), ap(s1), ap(s2), op0, op1), [a, s1, s2], [o])

    def scan(o, a, b, op0, op1):
        rec("v", lambda: g.vector.tensor_tensor_scan(ap(o), ap(a), ap(b), 0.0, op0, op1), [a, b], [o])

    def fill(o, c):
        rec("v", lambda: g.vector.memset(ap(o), c), [], [o])

    def turn(o, i):
        rec("v", lambda: g.vector.transpose(ap(o), ap(i)), [i], [o])

    def act(o, i, f, bias=0.0, scale=1.0):
        rec("a", lambda: g.scalar.activation(ap(o), ap(i), f, bias=ap(bias), scale=scale), [i, bias], [o])

    def mm(o, l, r, start, stop):
        rec("p", lambda: g.tensor.matmul(ap(o), ap(l), ap(r), start, stop), [l, r], [o])

    def load(qn, o, src, sem, after=()):
        e = g.sync if qn == "s" else g.scalar
        return rec(qn, lambda: e.dma_start(ap(o), src).then_inc(T.sem[sem], 16), [], [o], sem, 16, after)

    def store(qn, dst, i, sem):
        e = g.sync if qn == "s" else g.scalar
        return rec(qn, lambda: e.dma_start(dst, ap(i)).then_inc(T.sem[sem], 16), [i], [], sem, 16)

    sent, came = [0], {}

    def send(p, after=()):
        here, there = _sides(T, p, q)

        def caller(hops, before):
            def call():
                if p[0] == "c" and hops[0][2][0] == "a":
                    g.wait_ge(T.sem.sent, before)
                return g.remote_dma_fused([RemoteDMATransfer(
                    dst_ids=[_dst(topo, d, core) for d in ds], dma_engine_mask=_bits(e), remote_sem=T.sem[s],
                    srcs=[here], dsts=[here if s[0] == "h" else there for d in ds]) for ds, e, s in hops],
                    local_sem=T.sem.sent)
            return call
        go = None
        if p in LATE:
            after = list(after) + [came["x" + p[1]]]
        for hops in _first_hop(T, topo, q, p):
            before = sent[0]
            sent[0] += sum(len(e) for d, e, s in hops)
            rec("g", caller(hops, before), [vw("dx") if p == "x0" else vw(*_block(p, q))], [], "sent", -1, after)
            if p == "x0" and go is None:
                go = rec("g", lambda: g.sem_inc(T.sem.go, 1), [], [], "go", 1)
        came[p] = rec(None, None, [], [vw(*_block(p, s)) for s in range(NR) if s != q], "a" + p, _arrivals(T, topo, q, p))
        return go

    own = q * V
    load("s", vw("dx"), T.x0[:], "ld")
    load("a", vw("ei"), T.sc0[:], "le")
    load("s", vw("ca"), T.cas[:], "lc")
    load("a", vw("ti"), T.th[:], "lt")
    load("a", vw("ro"), T.rol[:], "lr")
    load("s", vw("fr", 0, F0), T.frm[:, 0:F0], "lf0")
    rec("g", lambda: g.iota(ap(vw("pi", 0, 1)), [[1, 1]], 0, 1), [], [vw("pi", 0, 1)])
    rec("g", lambda: g.iota(ap(vw("col", 0, 8)), [[1, 8]], 0, 0), [], [vw("col", 0, 8)])
    rec("g", lambda: g.iota(ap(vw("col", 8, 24)), [[1, 8], [0, 2]], 0, 0), [], [vw("col", 8, 24)])
    rec("g", lambda: g.iota(ap(vw("cf")), [[1, 144]], 0, 0, allow_small_or_imprecise_dtypes=True), [], [vw("cf")])
    go = send("x0")
    rec("g", lambda: g.iota(ap(vw("kb")), [[0, 8], [1, 16]], 0, 0, allow_small_or_imprecise_dtypes=True), [], [vw("kb")])

    P = vw("pi", 0, 1)
    ts(vw("pi", 1, 2), P, 15, OP.bitwise_and)
    ts(vw("pi", 2, 3), P, 7, OP.bitwise_and)
    ts(vw("pi", 3, 4), P, 3, OP.arith_shift_right, 1, OP.bitwise_and)
    ts(vw("pi", 4, 5), P, 16, OP.bitwise_and)
    ts(vw("pi", 5, 6), P, 112, OP.bitwise_and)
    cp(vw("pf", 0, 6), vw("pi", 0, 6))
    pP, pR, p7, p3, pG, pB = [vw("pf", i, i + 1) for i in range(6)]
    ts(vw("pf", 8, 9), p7, 16.0, OP.mult, p3, OP.add)
    ts(vw("pf", 9, 10), p7, 32.0, OP.mult, p3, OP.add)
    ts(vw("pf", 10, 11), pR, 8.0, OP.mult)
    ts(vw("pf", 11, 12), pR, pG, OP.add)
    act(vw("pf", 12, 13), pB, AF.Identity, bias=15.0)
    act(vw("pf", 13, 14), pB, AF.Identity, bias=7.5)
    c8 = vw("col", 0, 8)
    ts(vw("lu", 16, 32), vw("col", 8, 24), vw("pf", 10, 11), OP.add)
    ts(vw("lu", 32, 40), c8, 32.0, OP.mult, vw("pf", 11, 12), OP.add)
    ts(vw("lu", 8, 16), c8, 2.0, OP.mult, vw("pf", 9, 10), OP.add)
    ts(vw("lu", 0, 8), c8, 2.0, OP.mult, vw("pf", 8, 9), OP.add)
    PERM = vw("lu", 0, 8)
    PERMD = vw("lu", 8, 16)
    DUP = vw("lu", 16, 32)
    SEL = vw("lu", 32, 40)

    def scene_list(t):
        src = vw("ei", t, 16, 2) if t < 2 else vw("en0")
        cp(vw("sl", 16 * t, 16 * t + 16, 2), src)
        cp(vw("sl", 16 * t + 1, 16 * t + 16, 2), src)

    def frames_of(t):
        cp(vw("xf"), ind(vw("ro"), vw("sl", 16 * t, 16 * t + 16)))
        cp(vw("ofr", H * (t % 2), H * (t % 2) + H), ind(vw("xf"), PERMD))

    def frames_gather(t, lo, hi, on_vector=False):
        o, i = vw("yg", 16 * lo, 16 * hi), ind(vw("fr"), vw("ofr", H * (t % 2) + lo, H * (t % 2) + hi))
        if on_vector:
            cp(o, i)
        else:
            act(o, i, AF.Copy)

    def state(name, t):
        return vw(name, own + t, own + V, 2) if t < 2 else vw(name, UE + q * H, UE + q * H + H)

    def move(o, i, on_scalar):
        if on_scalar:
            act(o, i, AF.Copy)
        else:
            cp(o, i)

    def cast_rows(t):
        col = vw("cp", H * (t % 2), H * (t % 2) + H)
        if t == 0:
            cp(col, vw("ca", 0, V, 2))
        elif t == 1:
            n = vw("ca", 1, V, 2)
            ts(vw("u1"), n, 1, OP.bitwise_and)
            ts(vw("u4"), n, 0.5, OP.mult, float(UE), OP.add)
            ts(vw("u3"), vw("u1"), -4096.0, OP.mult, 4096.0, OP.add)
            tt(vw("u5"), vw("u3"), n, OP.add)
            tt(col, vw("u5"), vw("u4"), OP.min)
        else:
            n = state("ct", 2)
            ts(vw("u2"), n, 0.5, OP.mult, -0.25, OP.add)
            ts(vw("u4"), n, 1024.0, OP.mult)
            ts(vw("u3"), vw("u2"), -2047.0, OP.mult)
            tt(col, vw("u3"), vw("u4"), OP.add)
        move(vw("xc", V * (t % 2), V * (t % 2) + V), ind(col, DUP), t < 2)
        cp(vw("oxt", H * (t % 2), H * (t % 2) + H), col)

    def cast_turn(t):
        b = 264 * (t % 2)
        turn(vw("tc"), vw("xc", V * (t % 2), V * (t % 2) + V))
        move(vw("pw", b + 136, b + 264), ind(vw("tc"), SEL), t < 1)

    def frame_turn(t):
        b = 264 * (t % 2)
        turn(vw("tf"), vw("xf"))
        move(vw("pw", b + 8, b + 136), ind(vw("tf"), SEL), t < 1)

    def steps(t):
        b = 264 * (t % 2)
        tt(vw("dl", 256 * (t % 2), 256 * (t % 2) + 256), vw("pw", b + 7, b + 263), vw("pw", b + 8, b + 264), OP.subtract)

    def halves(t):
        act(vw("xoh"), state("xt", t), AF.Copy, scale=0.5)
        act(vw("xoq"), state("xt", t), AF.Identity, bias=-0.25, scale=0.5)

    def weights():
        c128, t1, t2 = vw("cf", 0, 128), vw("t1", 0, 128), vw("t2")
        act(vw("t1"), vw("cf"), AF.Abs, bias=vw("pf", 12, 13), scale=-1.0)
        act(vw("b16"), vw("t1"), AF.Relu, bias=KW, scale=-KW)
        act(t2, c128, AF.Abs, bias=pP, scale=-1.0)
        act(vw("eye", 0, 128), t2, AF.Relu, bias=1.0, scale=-1.0)
        act(vw("eye", 128, 256), vw("eye", 0, 128), AF.Copy, scale=-1.0)
        act(t1, c128, AF.Abs, bias=vw("pf", 13, 14), scale=-1.0)
        act(t2, t1, AF.Sign, bias=8.0, scale=-1.0)
        act(vw("gpw"), t2, AF.Relu, scale=256.0)
        act(vw("gmw"), vw("gpw"), AF.Copy, scale=-1.0)
        act(t2, vw("gpw"), AF.Copy, scale=16.0)
        act(t1, vw("eye", 0, 128), AF.Copy, scale=131072.0)
        act(vw("kp"), c128, AF.Copy, scale=1.0 / 128)
        fill(vw("ones"), 1.0)
        fill(vw("cst", 0, 128), -10.0)
        fill(vw("cst", 128, 256), -864.0)
        act(vw("cst", 256, 512), vw("cst", 0, 256), AF.Copy, scale=-1.0)

    def weights_end():
        tt(vw("vpw"), vw("t1", 0, 128), vw("t2"), OP.subtract)
        act(vw("vmw"), vw("vpw"), AF.Copy, scale=-1.0)

    def pick(k):
        return vw("b16", 15 - k, 143 - k)

    def distances(t):
        win = vw("xt", WIN[t][0], WIN[t][1])
        mm(vw("key", 0, H), vw("ones"), vw("kp"), True, False)
        mm(vw("key", 0, H), vw("kb"), vw("ones"), False, False)
        for i, n in enumerate(("gp", "vp", "gm", "vm")):
            mm(vw(n, 0, H), vw("ones"), vw("cst", 128 * i, 128 * i + 128), True, False)
        n = 16 * SA

        def sums(lo, hi, src):
            act(vw("ad", 16 * lo, 16 * hi), src, AF.Abs)
            for r in range(lo // 8, hi // 8):
                mm(vw("key", 0, H), pick(r), vw("ad", 128 * r, 128 * r + 128), False, r == 15)
        mm(vw("dp", 0, n), vw("eye", 128, 256), vw("yg", 0, n), True, False)
        act(vw("xg", 0, n), ind(win, vw("oxt", H * (t % 2), H * (t % 2) + SA)), AF.Copy)
        mm(vw("dp", 0, n), vw("eye", 0, 128), vw("xg", 0, n), False, True)
        for lo, hi in CHUNKS:
            tt(vw("df", 16 * lo, 16 * hi), ind(win, vw("oxt", H * (t % 2) + lo, H * (t % 2) + hi)),
               vw("yg", 16 * lo, 16 * hi), OP.subtract)
            sums(lo, hi, vw("df", 16 * lo, 16 * hi))
            if lo == SA:
                sums(0, SA, vw("dp", 0, n))
            for a, k0, k1 in ROLES.get(hi, []):
                for k in range(k0, k1):
                    mm(vw("dr", a, a + 64), pick(k), vw("ad", 16 * a + k, 16 * a + 1024, 16), k == 0, k == 15)

    def signs(t):
        act(vw("sg"), vw("dr", 0, H), AF.Sign, bias=vw("bias", t, t + 1), scale=1.0 / KW)
        order = ("gm", "gp", "vp", "vm", "jw") if t < 2 else ("vp", "vm", "jw", "gm", "gp")
        for n in order:
            if n != "jw":
                mm(vw(n, 0, H), vw(n + "w"), vw("sg"), False, True)
            else:
                for r in range(16):
                    mm(vw("jw", 0, 8), pick(r), vw("sg", 8 * r, 8 * r + 8), r == 0, r == 15)

    def carry(t, i):
        lo, d = 128 * i, 256 * (t % 2) + 128 * i
        scan(vw("zz", lo, lo + 128), vw("dl", d, d + 128), vw("nn"), OP.add, OP.mult)

    def best(t):
        b = 264 * (t % 2)
        tt(vw("bi"), vw("zz", 15, 256, 16), vw("pw", b + 23, b + 264, 16), OP.add)
        cp(vw("bu", 0, 16), vw("bi"))

    def cast_gather(t, on_scalar):
        move(vw("ccj"), ind(vw("ct", WIN[t][0], WIN[t][1]), vw("bu", 8, 16)), on_scalar)

    def features(t, out):
        gp, gm = vw("gp", 0, H), vw("gm", 0, H)
        scan(vw("mn"), vw("rst"), vw("key", 0, H), OP.add, OP.min)
        if t < 2:
            cp(vw("mi", 0, 8), vw("mn", 15, 128, 16))
            ts(vw("mi", 8, 16), vw("mi", 0, 8), 2047, OP.bitwise_and)
            cp(vw("bu", 16, 24), vw("mi", 8, 16))
            act(vw("ybj"), ind(vw("yg"), vw("bu", 16, 24)), AF.Copy, scale=0.5)
            signs(t)
            tt(vw("nn"), vw("mn"), vw("key", 0, H), OP.not_equal)
            carry(t, 1)
        else:
            tt(vw("nn"), vw("mn"), vw("key", 0, H), OP.not_equal)
            signs(t)
            carry(t, 0)
            carry(t, 1)
            best(t)
            act(vw("vps"), vw("vp", 0, H), AF.Copy)
            act(vw("ybj"), ind(vw("fr"), vw("bu", 0, 8)), AF.Copy, scale=0.5)
            cast_gather(t, True)

        def differ():
            tt(vw("ddh"), ind(vw("ybj"), PERM), vw("xoh"), OP.subtract)
            act(vw("aa"), vw("ddh"), AF.Abs, scale=2.0)
            if t < 2:
                act(vw("vps"), vw("vp", 0, H), AF.Copy)
        return [differ,
                lambda: tt(vw("hh"), ind(vw("ybj"), PERM), vw("xoq"), OP.add),
                lambda: tt(vw("p2"), vw("aa"), gm, OP.min),
                lambda: tt(gp, vw("hh"), gp, OP.min),
                lambda: tt(out, vw("p2"), gp, OP.max)]

    def casts(t, out):
        vm = vw("vm", 0, H)
        return ([lambda: tt(vm, state("ct", t), vm, OP.min)] + ([lambda: cast_gather(t, False)] if t < 2 else [])
                + [lambda: tt(vw("q1"), ind(vw("ccj"), PERM), vw("vps"), OP.min),
                   lambda: tt(out, vw("q1"), vm, OP.max)])

    def scenes(t, out):
        nxt = vw("e1", t, 16, 2) if t < 2 else vw("e1", 40, 48)

        def low():
            if t < 2:
                carry(t, 0)
                best(t)
            ts(vw("fm"), vw("bi", 0, 8), 1023, OP.bitwise_and)

        def flag():
            ts(vw("j01"), vw("jw", 0, 8), 5 * KW, OP.is_gt)
            if t < 2:
                mm(vw("jw", 8, 16), vw("ones"), vw("j01"), True, True)
        return [low, flag,
                lambda: tt(vw("ed", 0, 8), vw("fm"), nxt, OP.subtract),
                lambda: tt(vw("ed", 8, 16), vw("ed", 0, 8), vw("j01"), OP.mult),
                lambda: tt(out, vw("ed", 8, 16), nxt, OP.add)]

    def run(calls):
        for c in calls:
            c()

    def weave(first, second):
        runs = []
        for calls in (first, second):
            n = len(ops)
            run(calls)
            runs.append(ops[n:])
            del ops[n:]
        for i in range(max(len(r) for r in runs)):
            for r in runs:
                ops.extend(r[i:i + 1])

    def jumps(t):
        rec("v", lambda: g.vector.tensor_reduce(ap(vw("as1")), ap(vw("jw", 8, 16)), AxisListType.X, OP.add),
            [vw("jw", 8, 16)], [vw("as1")])
        cp(vw("ai", 0, 1), vw("as1"))
        ts(vw("ai", 1, 2), vw("ai", 0, 1), 127, OP.bitwise_and)
        ts(vw("bias", t + 1, t + 2), vw("ai", 1, 2), -1.0, OP.mult, vw("bias", 0, 1), OP.add)

    fill(vw("pw", 0, 8), 0.0)
    fill(vw("pw", 264, 272), 0.0)
    weights()
    ts(vw("e1", 16, 32), vw("ei"), 1.0, OP.add)
    ts(vw("bias", 0, 1), vw("ti"), -1.0, OP.mult, -0.5, OP.add)
    ts(vw("e1", 0, 16), vw("e1", 16, 32), 1023, OP.bitwise_and)
    scene_list(0)
    scene_list(1)
    cast_rows(0)
    cast_rows(1)
    weights_end()
    cast_turn(0)
    cp(vw("ct", own, own + V), vw("ca"))
    load("s", vw("xt", own, own + V), T.x0[:], "lx", [go])
    frl = load("s", vw("fr", F0, FCUT), T.frm[:, F0:FCUT], "lf1")
    load("s", vw("fr", FCUT, 4096), T.frm[:, FCUT:4096], "lf2")
    send("c0", [frl])
    frames_of(0)
    frame_turn(0)
    frames_of(1)
    steps(0)
    act(vw("rst"), vw("kb"), AF.Relu, bias=8192 * KW, scale=-8192 * KW)
    halves(0)
    frames_gather(0, 0, YV, True)
    for lo, hi in ((YV, 48), (48, 72), (72, 96), (96, H)):
        frames_gather(0, lo, hi)

    distances(0)
    run(features(0, vw(*_block("x1", q))))
    send("x1")
    frames_gather(1, 0, YV)
    frames_gather(1, YV, H)
    halves(1)
    fe = scenes(0, vw("en0"))
    run(fe[:1])
    weave([lambda: run(casts(0, vw(*_block("c1", q)))), lambda: send("c1"), lambda: cast_turn(1), lambda: frame_turn(1)],
          [lambda: run(fe[1:]), lambda: jumps(0), lambda: scene_list(2)])
    weave([lambda: frames_of(2), lambda: steps(1)],
          [lambda: ts(vw("e1", 32, 40), vw("en0"), 1.0, OP.add),
           lambda: ts(vw("e1", 40, 48), vw("e1", 32, 40), 1023, OP.bitwise_and)])

    distances(1)
    run(features(1, vw(*_block("x2", q))))
    send("x2")
    frames_gather(2, 0, YV)
    frames_gather(2, YV, H)
    halves(2)
    fe = scenes(1, vw("oute", 1, 16, 2))
    run(fe[:1])
    weave([lambda: run(casts(1, vw(*_block("c2", q)))), lambda: send("c2"), lambda: cast_rows(2)],
          [lambda: run(fe[1:]), lambda: jumps(1), lambda: frame_turn(2)])
    cast_turn(2)
    steps(2)
    act(vw("outx", 1, V, 2), vw(*_block("x2", q)), AF.Copy)
    act(vw("outc", 1, V, 2), vw(*_block("c2", q)), AF.Copy)

    distances(2)
    fx = features(2, vw("outx", 0, V, 2))
    fc, fe = casts(2, vw("outc", 0, V, 2)), scenes(2, vw("oute", 0, 16, 2))
    run([fe[0], fc[0], fe[2], fx[0], fx[1], fe[1], fc[1], fe[3], fx[2], fe[4]])
    s1 = store("s", T.ye[:], vw("oute"), "oe")
    run([fc[2]])
    s2 = store("a", T.yc[:], vw("outc"), "oc")
    run([fx[3], fx[4]])
    s3 = store("s", T.yx[:], vw("outx"), "ox")
    rec("s", lambda: None, [], [], "end", 0, [s1, s2, s3])
    _emit(ops, g, T)
    g.wait_ge(T.sem.sent, sent[0])
